import numpy as np, ml_dtypes
CORES = [3,11,19,27,35,43,51,59]
N = 8
BF = ml_dtypes.bfloat16
def gentries(a):
    return np.ascontiguousarray(a.reshape(8, 16, -1).transpose(0, 2, 1)).reshape(8, -1)
def gtable(e):
    e = np.asarray(e); return np.ascontiguousarray(e.reshape(8, -1, 16).transpose(0, 2, 1)).reshape(128, -1).astype(np.int32)
V, DV, M, DC, IT, CAP, B = 256, 4, 128, 8, 2, 160, 51
E = V * DV
def mixed(rng):
    c = np.full((N, N), E // N)
    for i in range(6 * N):
        p, p2 = rng.permutation(N)[:2]; q, q2 = rng.permutation(N)[:2]
        t = rng.integers(0, min(c[p, q2], c[p2, q], CAP - c[p, q], CAP - c[p2, q2]) + 1)
        c[p, q] += t; c[p2, q2] += t; c[p, q2] -= t; c[p2, q] -= t
    return c
def fullest(rng):
    odd = np.add.outer(rng.permutation(N), rng.permutation(N)) % 2
    return E // N + (CAP - E // N) * (1 - 2 * odd)
def fewest(rng):
    low = max(0, E - (N - 1) * CAP); each = (E - low) // (N - 1); more = E - low - each * (N - 1)
    w = np.concatenate([[low], each + (np.arange(N - 1) < more)]); k = rng.integers(1, N); p = np.arange(N)
    c = np.zeros((N, N), np.int64)
    for i in range(N): c[p, (p + k + i) % N] = w[i]
    return c
def graph(rng, ways, near=False, holes=False):
    sn = rng.integers(0, V, (N, 8, N * CAP)); pl = np.zeros((N, 8, E), np.int64); vl = np.zeros((N, 8, E), np.int64)
    def order(n, d):
        return np.add.outer(rng.permutation(n), n * np.arange(d)).reshape(-1) if near else rng.permutation(n * d)
    ve = [[order(V, DV) for r in range(N)] for g in range(8)]; ce = [[order(M, DC) for r in range(N)] for g in range(8)]
    c = ways(rng); va = np.add.accumulate(c, axis=1) - c; ca = np.add.accumulate(c, axis=0) - c
    for g in range(8):
        for p in range(N):
            for q in range(N):
                h = (g + p * q) % 8; n = int(c[p, q]); s = rng.permutation(CAP if holes else n)[:n]
                a = ve[g][p][va[p, q]:va[p, q] + n]; b = ce[h][q][ca[p, q]:ca[p, q] + n]
                vl[p, g, a] = q * CAP + s; pl[q, h, b] = p * CAP + s; sn[p, g, q * CAP + s] = a % V
    return {"sn": np.stack([gtable(e) for e in sn]), "pl": np.stack([gtable(e) for e in pl]), "vl": np.stack([gtable(e) for e in vl])}
def heard(rng):
    k = np.stack([rng.permutation(16) for g in range(8)]).reshape(1, 128, 1)
    mean = B * np.array([0, 0.1, 0.2, 0.7])[k // 4]; noise = B * np.array([0.1, 0.2, 0.4, 0.6])[k % 4]
    return (np.clip(np.rint(mean + noise * rng.standard_normal((N, 128, V))), -B, B) + 0.0).astype(BF)
def setup_inputs(rng):
    return {"x": heard(rng), **graph(rng, mixed)}
def setup_inputs_full(rng):
    return {"x": heard(rng), **graph(rng, fullest)}
def setup_inputs_holes(rng):
    return {"x": heard(rng), **graph(rng, fewest, holes=True)}
def setup_inputs_ties(rng):
    k = np.stack([rng.permutation(16) for g in range(8)]).reshape(1, 128, 1) % 4; z = (N, 128, V)
    sg = 2 * rng.integers(0, 2, z) - 1
    v = np.where(k == 0, sg, np.where(k == 1, rng.integers(-2, 3, z), np.where(k == 2, np.where(rng.random(z) < 0.1, -B, B), np.where(rng.random(z) < 0.0625, 0, B * sg))))
    return {"x": v.astype(BF), **graph(rng, mixed)}
def setup_inputs_twins(rng):
    return {"x": heard(rng), **graph(rng, mixed, near=True)}
def setup_inputs_spread(rng):
    hi = B >> rng.integers(0, 6, (N, 128, 1)); hi[:, ::16] = B
    v = rng.integers(-hi, hi + 1, (N, 128, V)) * (rng.random((N, 1, V)) > 0.0625)
    return {"x": v.astype(BF), **graph(rng, mixed, holes=True)}
def check_inputs(d):
    bad = []
    try:
        x = np.asarray(d["x"]).astype(np.float64)
        if not (np.isfinite(x).all() and (x == np.rint(x)).all() and (np.abs(x) <= B).all()): bad.append("x is whole and within B")
        sn, pl, vl = [np.stack([gentries(np.asarray(d[k][r])) for r in range(N)]).astype(np.int64) for k in ("sn", "pl", "vl")]
        if sn.min() < 0 or sn.max() >= V: bad.append("sn in range")
        if min(pl.min(), vl.min()) < 0 or max(pl.max(), vl.max()) >= N * CAP: return bad + ["pl and vl in range"]
        name = True; v = np.arange(E) % V
        uv = np.zeros((8, N, N * CAP), np.int64); uc = np.zeros((8, N, N * CAP), np.int64)
        for g in range(8):
            for r in range(N):
                uv[g, r] = np.bincount(vl[r, g], minlength=N * CAP); uc[g, r] = np.bincount(pl[r, g], minlength=N * CAP)
                name = name and bool((sn[r, g][vl[r, g]] == v).all())
        a = np.arange(N); h = (np.arange(8)[:, None, None] + np.multiply.outer(a, a)) % 8
        there = uc.reshape(8, N, N, CAP).transpose(0, 2, 1, 3)[h, a[:, None], a] > 0
        if max(uv.max(), uc.max()) > 1: bad.append("entries of pl and of vl differ")
        if not ((uv.reshape(8, N, N, CAP) > 0) == there).all(): bad.append("vl and pl name the same slots")
        if not name: bad.append("sn names the variable of each slot")
    except Exception:
        bad.append("shapes")
    return bad
def reference(x, sn, pl, vl):
    g = np.arange(8)[:, None, None]; r = np.arange(N)[:, None]
    ve = np.stack([gentries(vl[p]).astype(np.int64) for p in range(N)], axis=1) + (g * N + r) * N * CAP
    k = np.stack([gentries(pl[q]).astype(np.int64) for q in range(N)], axis=1); p = k // CAP
    ce = (((g - p * r) % 8 * N + p) * N + r) * CAP + k % CAP
    u = x.astype(np.float32).astype(np.int64).reshape(N, 8, 16, V).transpose(2, 1, 0, 3)
    back = np.zeros((16, 8 * N * N * CAP), np.int64); there = np.zeros((16, 8 * N * N * CAP), np.int64); tot = u
    for i in range(IT):
        there[:, ve] = np.clip(np.tile(tot, (1, 1, 1, DV)) - back[:, ve], -B, B)
        m = there[:, ce].reshape(16, 8, N, DC, M); size = np.abs(m); neg = (m < 0).astype(np.int64); new = np.zeros_like(m)
        for e in range(DC):
            o = [j for j in range(DC) if j != e]
            new[:, :, :, e] = np.min(size[:, :, :, o], axis=3) * (1 - 2 * (np.add.reduce(neg[:, :, :, o], axis=3) % 2))
        back[:, ce] = new.reshape(16, 8, N, E)
        tot = u + np.add.reduce(back[:, ve].reshape(16, 8, N, DV, V), axis=3)
    return {"y": np.ascontiguousarray(tot.transpose(2, 1, 0, 3)).reshape(N, 128, V).astype(np.float32)}

@@ -1,0 +1,394 @@
+from concourse.bass import DstId, RemoteDMATransfer
+from concourse.mybir import dt, AluOpType, AxisListType, ActivationFunctionType
+
+NR, CAP, V, M = 8, 160, 256, 128
+W = NR * CAP
+BK = 2 * CAP
+H = 2 * BK
+NJ = 9 * M
+NH = NJ // 2
+B = 51.0
+OFF = 64
+OP = AluOpType
+AF = ActivationFunctionType
+RAW = 5
+TO_CHECKS = {"V": "g7 g4 g1 g0", "A": "g3 g2 g6 c4 c1", "recv": "V0 A5 V7 A3 V2 A6",
+             "calls": [[(5, 0, 8)], [(7, 0, 4), (3, 4, 4)], [(6, 0, 4), (2, 4, 4)], [(4, 0, 4), (1, 4, 4)]]}
+TO_VARS = {"V": "g7 g5 g4 g1 g0", "A": "g3 g2 g6 c5 c4 c1", "recv": "A0 V3 V7 V2 V6",
+           "calls": [[(3, 0, 8)], [(7, 0, 4), (2, 4, 4)], [(6, 0, 4), (5, 4, 4)], [(4, 0, 4), (1, 4, 4)]]}
+PLAN = {0: dict(TO_CHECKS, recv="V0 A7 A3 V5 V2 A6"), 1: TO_VARS, 2: TO_CHECKS, 3: TO_VARS}
+
+SCRATCH = {
+    "sn32": ("sbuf", [128, 80], "int32"), "pl32": ("sbuf", [128, 64], "int32"), "vl32": ("sbuf", [128, 64], "int32"),
+    "sn16": ("sbuf", [128, 80], "uint16"), "pl16": ("sbuf", [128, 64], "uint16"), "vl16": ("sbuf", [128, 64], "uint16"),
+    "rn32": ("sbuf", [128, 10], "int32"), "rn16": ("sbuf", [128, 10], "uint16"),
+    "ta": ("sbuf", [128, 64], "int32"), "tb": ("sbuf", [128, 64], "int32"), "tc": ("sbuf", [128, 64], "int32"),
+    "td": ("sbuf", [128, 64], "int32"), "pc16": ("sbuf", [128, 64], "uint16"),
+    "num": ("sbuf", [128, 512], "float32"), "num2": ("sbuf", [128, 512], "float32"),
+    "iva": ("sbuf", [128, W], "float32"), "ivb": ("sbuf", [128, W], "float32"),
+    "inv32": ("sbuf", [128, 80], "float32"), "inv16": ("sbuf", [128, 80], "uint16"),
+    "one": ("sbuf", [128, 256], "bfloat16"), "E": ("sbuf", [128, 256], "bfloat16"), "NI": ("sbuf", [128, 128], "bfloat16"),
+    "xs": ("sbuf", [128, 256], "bfloat16"), "Tw": ("sbuf", [128, 256], "bfloat16"), "ys": ("sbuf", [128, 256], "float32"),
+    "D": ("sbuf", [128, NJ], "bfloat16"), "A": ("sbuf", [128, NJ], "bfloat16"), "NA": ("sbuf", [128, NJ], "bfloat16"),
+    "F": ("sbuf", [128, NJ], "bfloat16"), "Z": ("sbuf", [128, NH], "bfloat16"),
+    "C0": ("sbuf", [128, 2 * NJ], "bfloat16"), "C1": ("sbuf", [128, 2 * NJ], "bfloat16"), "C2": ("sbuf", [128, 2 * NJ], "bfloat16"),
+    "sc": ("sbuf", [128, H], "bfloat16"), "so": ("sbuf", [128, H], "bfloat16"), "Rf": ("sbuf", [128, H], "bfloat16"),
+}
+for _d in range(NR):
+    SCRATCH["bk%d" % _d] = ("psum", [128, 512], "float32")
+for _r in range(2):
+    for _n, _w in (("Tg", W), ("Rs", W), ("Lm", W), ("Lr", W), ("Xm", W), ("Xr", W), ("Dw", W), ("Rv", W), ("Gv", 1024), ("sv", H),
+                   ("rx", 256)):
+        SCRATCH["%s%d" % (_n, _r)] = ("sbuf", [128, _w], "bfloat16")
+SEMAPHORES = ["sV", "sA", "sP", "sG", "dx", "dsn", "dpl", "dvl", "df", "dr", "da", "dy", "ls", "rn"]
+SEMAPHORES += ["arr%d_%d" % (ph, p) for ph in range(4) for p in range(NR)]
+
+
+def rank_program(g, core, T, topo):
+    me = T.rank_of(core)
+    if me is None:
+        return
+    queue = {"V": g.vector, "A": g.scalar, "P": g.tensor, "G": g, "S": g.sync}
+    cnt = {"V": 0, "A": 0, "P": 0, "G": 0, "ls": 0}
+    seen = {}
+    vec, act, ten = g.vector, g.scalar, g.tensor
+
+    def need(q, *toks):
+        for sem, val in toks:
+            if seen.get((q, sem), 0) < val:
+                queue[q].wait_ge(T.sem[sem], val)
+                seen[(q, sem)] = val
+
+    def run(q, inst):
+        cnt[q] += 1
+        inst.then_inc(T.sem["s" + q], 1)
+        return ("s" + q, cnt[q])
+
+    s0 = me // 2
+    same = [s0, s0 ^ 2]
+    diff = [s0 ^ 1, s0 ^ 3]
+
+    def bank(buf, b):
+        return buf[:, b * BK:(b + 1) * BK]
+
+    def blk(buf, q):
+        return buf[:, q * CAP:(q + 1) * CAP]
+
+    def half(buf, q):
+        b = q // 2
+        return blk(buf, 2 * (same.index(b) if b in same else diff.index(b)) + q % 2)
+
+    def ps(d):
+        return T["bk%d" % d][:, 0:CAP]
+
+    def turn(ph, r):
+        k = me * r if ph % 2 == 0 else -me * r
+        s = (128 - 16 * (k % 8)) % 128
+        return T.E[:, s:s + 128]
+
+    def const(ap, n, value):
+        return run("G", g.iota(ap, [[0, n]], value, 0, allow_small_or_imprecise_dtypes=True))
+
+    eye = T.E[:, 0:128]
+    g.sync.dma_start(T.sn32[:, :], T.sn[:, :]).then_inc(T.sem.dsn, 16)
+    act.dma_start(T.xs[:, :], T.x[:, :]).then_inc(T.sem.dx, 16)
+    g.sync.dma_start(T.pl32[:, :], T.pl[:, :]).then_inc(T.sem.dpl, 16)
+    act.dma_start(T.vl32[:, :], T.vl[:, :]).then_inc(T.sem.dvl, 16)
+    sn_in, x_in, pl_in, vl_in = ("dsn", 16), ("dx", 16), ("dpl", 16), ("dvl", 16)
+    num = run("G", g.iota(T.num[:, :], [[2, 4], [18, 128]], 1 + OFF, 0, allow_small_or_imprecise_dtypes=True))
+    ones = run("V", vec.memset(T.one[:, :], 1.0))
+    need("G", ones)
+    eyes = run("G", g.affine_select(T.E[:, :], T.one[:, :], [[0, 2], [-1, 128]], OP.is_equal, 0.0, 0, 1))
+    need("A", ones)
+    run("A", act.activation(T.C1[:, 1:2 * NJ:NJ], T.one[:, 0:2], AF.Silu, bias=B - 1.0))
+    zero = run("V", vec.memset(T.Z[:, :], 0.0))
+    fill = run("V", vec.memset(T.iva[:, :], 0.0))
+    need("S", fill)
+    g.sync.dma_start(T.ivb[0:128:16, :], T.iva[0:128:16, :]).then_inc(T.sem.df, 16)
+    need("V", sn_in)
+    sn16 = run("V", vec.tensor_copy(T.sn16[:, :], T.sn32[:, :]))
+
+    def toks(ph, name, kind=None):
+        return [(t[0], int(t[1:])) for t in PLAN[ph][name].split() if kind is None or t[0] == kind]
+
+    def turned_here(ph):
+        return [d for q in "VA" for k, d in toks(ph, q, "c")]
+
+    def arrived(ph, d):
+        return ("arr%d_%d" % (ph, me ^ d), [n for c in PLAN[ph]["calls"] for e, o, n in c if e == d][0])
+
+    def send(items):
+        tr = []
+        for d, o, n, src, dst, sem in items:
+            to = T.cores[me ^ d]
+            rid, pid, _s = topo.addr(to)
+            tr.append(RemoteDMATransfer(dst_ids=[DstId(rid=rid, pnc=pid)], dma_engine_mask=sum(1 << e for e in topo.engines(core, to)[o:o + n]),
+                                        remote_sem=T.sem[sem], src=src, dst=dst))
+            cnt["ls"] += n
+        g.remote_dma_fused(tr, local_sem=T.sem.ls)
+
+    def send_raw(ph, win):
+        d, o, n = PLAN[ph]["calls"][0][0]
+        send([(d, o, n, win[:, :], T["rx%d" % (ph // 2)][:, :], "arr%d_%d" % (ph, me))])
+
+    def drain(ph, q, out, src):
+        if ph % 2 == 0:
+            if q == "V":
+                return run("V", vec.tensor_scalar(out, src, 2.0, 1.0, OP.mult, OP.add))
+            return run("A", act.activation(out, src, AF.Identity, bias=1.0, scale=2.0))
+        if q == "V":
+            return run("V", vec.tensor_copy(out, src))
+        return run("A", act.activation(out, src, AF.Copy))
+
+    def by_slots(ph, win, lst, bufs, ready):
+        src, land, xsrc, xland = bufs
+        xs, got, out, trn = turned_here(ph), {}, {}, {}
+        need("V", *ready)
+        need("A", *ready)
+
+        def gather(q, d):
+            r = me ^ d
+            i, o = win.indirect(lst[:, r * CAP // 16:(r + 1) * CAP // 16]), blk(src, r)
+            if q == "A":
+                return run("A", act.activation(o, i, AF.Copy))
+            if ph == 2 and not d & 2:
+                return run("V", vec.tensor_tensor(o, i, blk(T.Rv0, r), OP.subtract))
+            if ph % 2 and not d & 2:
+                return run("V", vec.tensor_tensor(o, i, half(T.sc, r), OP.mult))
+            return run("V", vec.tensor_copy(o, i))
+
+        todo = {q: toks(ph, q) for q in "VA"}
+        while todo["V"] or todo["A"]:
+            for q in "VA":
+                while todo[q] and (todo[q][0][0] == "g" or todo[q][0][1] in trn):
+                    kind, d = todo[q].pop(0)
+                    r = me ^ d
+                    if kind == "c":
+                        need(q, trn[d])
+                        out[d] = drain(ph, q, blk(xsrc, r), ps(d))
+                        continue
+                    got[d] = gather(q, d)
+                    if d in xs:
+                        need("P", eyes, got[d])
+                        trn[d] = run("P", ten.matmul(ps(d), turn(ph, r), blk(src, r), True, True))
+        for c in PLAN[ph]["calls"][(ph + 1) % 2:]:
+            for d, o, n in c:
+                need("G", out[d] if d in xs else got[d])
+            send([(d, o, n, blk(xsrc if d in xs else src, me ^ d), blk(xland if d in xs else land, me), "arr%d_%d" % (ph, me))
+                  for d, o, n in c])
+        return got
+
+    def taken(ph, mine, mine_ready, land, rv, early=None):
+        done, ev, left = {}, {}, [early] if early else []
+        for q, d in toks(ph, "recv"):
+            p = me ^ d
+            need("P", rawg[ph] if (ph, d) in ((0, RAW), (2, RAW)) else arrived(ph, d) if d else mine_ready)
+            done[d] = run("P", ten.matmul(ps(d), turn(ph, p), blk(land if d else mine, p), not (ph == 2 and (d & 2 or d == RAW)), True))
+            if left:
+                left.pop()()
+        for q, d in toks(ph, "recv"):
+            p = me ^ d
+            need(q, done[d])
+            if ph % 2 and d & 2:
+                need("V", sv[0])
+                ev[d] = run("V", vec.tensor_tensor(blk(rv, p), ps(d), half(T["sv%d" % (ph // 2)], p), OP.mult))
+            else:
+                ev[d] = drain(ph, q, blk(rv, p), ps(d))
+        for d in turned_here(ph):
+            ev[d] = arrived(ph, d)
+        return ev
+
+    def gather_raw(ph):
+        need("V", arrived(ph, RAW))
+        win = T["rx%d" % (ph // 2)][:, 0:256]
+        rawg[ph] = run("V", vec.tensor_copy(blk(T["Lm%d" % (ph // 2)], me ^ RAW), win.indirect(T.rn16[:, :])))
+
+    inv, rf, sv, ni, rawg = [None], [None], [None], [None], {}
+    need("G", x_in)
+    send_raw(0, T.xs)
+    need("G", sn_in)
+    send([(RAW, 0, 8, T.sn32[:, (me ^ RAW) * 10:(me ^ RAW) * 10 + 10], T.rn32[:, :], "rn")])
+    own = by_slots(0, T.xs[:, 0:256], T.sn16, (T.Tg0, T.Lm0, T.Xm0, T.Dw0), [sn16, x_in])[0]
+    need("A", num)
+    num2 = run("A", act.activation(T.num2[:, :], T.num[:, :], AF.Silu, bias=8.0))
+    need("V", pl_in)
+    ta = run("V", vec.tensor_scalar(T.ta[:, :], T.pl32[:, :], 15, None, OP.bitwise_and))
+    tb = run("V", vec.tensor_scalar(T.tb[:, :], T.pl32[:, :], 4, None, OP.arith_shift_right))
+    need("V", ta)
+    tc = run("V", vec.tensor_scalar(T.tc[:, :], T.ta[:, :], 80.0, None, OP.mult))
+    pl16 = run("V", vec.tensor_copy(T.pl16[:, :], T.pl32[:, :]))
+    need("V", tb, tc)
+    td = run("V", vec.tensor_tensor(T.td[:, :], T.tc[:, :], T.tb[:, :], OP.add))
+    need("V", vl_in)
+    vl16 = run("V", vec.tensor_copy(T.vl16[:, :], T.vl32[:, :]))
+    need("V", td)
+    pc = run("V", vec.tensor_copy(T.pc16[:, :], T.td[:, :]))
+    need("V", pc, fill, num, ("df", 16))
+    scat = run("V", vec.tensor_copy(T.iva[:, 0:W].indirect(T.pc16[:, 0:32]), T.num[:, :]))
+    need("A", pc, num2, ("df", 16))
+    scat2 = run("A", act.activation(T.ivb[:, 0:W].indirect(T.pc16[:, 32:64]), T.num2[:, :], AF.Silu))
+    need("S", scat)
+    g.sync.dma_start(T.inv32[:, :], T.iva[0:128:16, :]).then_inc(T.sem.dr, 16)
+    need("V", ("rn", 8))
+    rn16 = run("V", vec.tensor_copy(T.rn16[:, :], T.rn32[:, :]))
+    need("V", rn16)
+    gather_raw(0)
+    need("G", zero)
+    const(T.Z[:, 8:NH:9], M // 2, int(B))
+    const(T.D[:, 8:NJ:9], M, 0)
+    z = const(T.C1[:, NJ - 2:2 * NJ:NJ], 2, 0)
+    c0 = {k: const(T.C0[:, k * NJ:(k + 1) * NJ:2], NH, 64) for k in (1, 0)}
+    need("G", scat2, ("dr", 16))
+    g.dma_start(T.inv32[:, :], T.ivb[0:128:16, :], accum_op=OP.add).then_inc(T.sem.da, 16)
+
+    def less_own(ds):
+        need("P", ni[0], rf[0])
+        for d in ds:
+            run("P", ten.matmul(ps(d), T.NI[:, :], half(T.Rf, me ^ d) if d & 2 else blk(T.Rs0, me ^ d), True, False))
+
+    def check(r, mine_ready):
+        dwin = T["Dw%d" % r]
+
+        def late():
+            need("P", sv[0])
+            less_own((6, 7))
+
+        ev = taken(2 * r, T["Tg%d" % r], mine_ready, T["Lm%d" % r], dwin, late if r else None)
+        win = dwin[:, 0:W]
+        need("V", pl16, *ev.values())
+        need("A", pl16, *ev.values())
+        for e in range(4):
+            gv = run("V", vec.tensor_copy(T.D[:, e:NJ:9], win.indirect(T.pl16[:, 8 * e:8 * e + 8])))
+            ga = run("A", act.activation(T.D[:, e + 4:NJ:9], win.indirect(T.pl16[:, 8 * e + 32:8 * e + 40]), AF.Copy))
+        need("V", gv, ga, z)
+        need("A", gv, ga, z)
+
+        def part(buf, k):
+            return buf[:, k * NH:(k + 1) * NH]
+
+        ab, na, lim, neg, suf, w, fs, f, pre = {}, {}, {}, {}, {}, {}, {}, {}, {}
+        for k in (1, 0):
+            f[k] = run("V", vec.tensor_tensor_scan(part(T.F, k), part(T.D, k), T.Z[:, :], B, OP.mult, OP.add))
+            ab[k] = run("A", act.activation(part(T.A, k), part(T.D, k), AF.Abs, bias=-0.5, scale=0.5))
+
+        def before(k):
+            need("V", ab[k])
+            lo, hi = k * NH + 1, (k + 1) * NH
+            pre[k] = run("V", vec.tensor_tensor_scan(T.C1[:, 2 * lo + 1:2 * hi:2], T.A[:, lo - 1:hi - 1], T.Z[:, :NH - 1], B, OP.min, OP.max))
+
+        def negative(k):
+            lo, hi = k * NH + 1, (k + 1) * NH
+            need("A", pre[k], c0[k])
+            neg[k] = run("A", act.activation(T.C0[:, 2 * lo - 1:2 * hi:2], T.C1[:, 2 * lo - 1:2 * hi:2], AF.Copy, scale=-1.0))
+
+        def negate(k):
+            if k:
+                need("V", ab[k])
+                na[k] = run("V", vec.tensor_scalar(part(T.NA, k), part(T.A, k), -1.0, None, OP.mult))
+            else:
+                need("A", ab[k])
+                na[k] = run("A", act.activation(part(T.NA, k), part(T.A, k), AF.Copy, scale=-1.0))
+
+        def limit(k):
+            need("G", na[k])
+            lim[k] = const(T.NA[:, k * NH + 8:(k + 1) * NH:9], M // 2, 64)
+
+        def start(k):
+            lo, hi = k * NH, (k + 1) * NH
+            need("V", f[k], na[k], pre[k])
+            fs[k] = run("V", vec.tensor_copy(T.A[:, lo + 8:hi:9], T.F[:, lo + 7:hi:9]))
+
+        def behind(k):
+            need("V", fs[k], lim[k])
+            top = (k + 1) * NH - 1
+            cols, to = slice(top, k * NH, -1), slice(2 * (top - 1), 2 * k * NH - 2 if k else None, -2)
+            suf[k] = run("V", vec.tensor_tensor_scan(T.C1[:, to], T.NA[:, cols], T.A[:, cols], 0.0, OP.max, OP.min))
+
+        def both(k):
+            need("V", suf[k], neg[k])
+            c = slice(2 * k * NH, 2 * (k + 1) * NH)
+            w[k] = run("V", vec.tensor_tensor_scan(T.C2[:, c], T.C0[:, c], T.C1[:, c], 0.0, OP.max, OP.min))
+
+        negate(0)
+        negate(1)
+        before(1)
+        limit(1)
+        negative(1)
+        before(0)
+        limit(0)
+        negative(0)
+        start(1)
+        behind(1)
+        start(0)
+        behind(0)
+        both(1)
+        if r == 0:
+            need("V", ("da", 16))
+            inv[0] = run("V", vec.tensor_scalar(T.inv16[:, :], T.inv32[:, :], 0.25 - OFF, 0.0, OP.add, OP.max))
+        both(0)
+        for i in range(2):
+            sc = run("A", act.activation(bank(T.sc, i), bank(dwin, same[i]), AF.Sign))
+        dst = T["Rs%d" % r]
+        got = by_slots(2 * r + 1, T.C2[:, 0:2 * NJ], T.inv16, (dst, T["Lr%d" % r], T["Xr%d" % r], T["Rv%d" % r]), [w[1], w[0], inv[0], sc])
+        if r == 0:
+            for i in range(2):
+                so = run("A", act.activation(bank(T.so, i), bank(dwin, diff[i]), AF.Sign))
+            for i in range(2):
+                sv[0] = run("A", act.activation(bank(T.sv0, i), bank(T.Tg0, diff[i]), AF.Sign, bias=0.5))
+            need("A", eyes)
+            ni[0] = run("A", act.activation(T.NI[:, :], eye, AF.Copy, scale=-1.0))
+            need("V", so, *got.values())
+            for i in range(2):
+                rf[0] = run("V", vec.tensor_tensor(bank(T.Rf, i), bank(dst, diff[i]), bank(T.so, i), OP.mult))
+        return got[0]
+
+    def variables(r, rs, out):
+        rv = T["Rv%d" % r]
+        ev = taken(2 * r + 1, T["Rs%d" % r], rs, T["Lr%d" % r], rv)
+        gd = T["Gv%d" % r]
+        need("V", vl16, *ev.values())
+        need("A", vl16, *ev.values())
+
+        def piece(d, lo=0, hi=256):
+            return gd[:, 256 * d + lo:256 * d + hi], rv[:, 0:W].indirect(T.vl16[:, 16 * d + lo // 16:16 * d + hi // 16])
+
+        o, i = piece(0)
+        g0 = run("V", vec.tensor_tensor(o, i, T.xs[:, :], OP.add))
+        g3 = [run("V", vec.tensor_copy(*piece(3, 128, 256)))]
+        g2 = run("A", act.activation(*piece(2), AF.Copy))
+        g3.append(run("A", act.activation(*piece(3, 0, 128), AF.Copy)))
+        need("V", g0)
+        o, i = piece(1)
+        g1 = run("V", vec.tensor_tensor(o, i, gd[:, 0:256], OP.add))
+        tt = T.bk0[:, 0:256]
+        need("P", ev[0], g2)
+        run("P", ten.matmul(tt, eye, gd[:, 512:768], True, False))
+        need("P", *g3)
+        t = run("P", ten.matmul(tt, eye, gd[:, 768:1024], False, True))
+        need("V", g1, t)
+        return run("V", vec.tensor_tensor(out[:, :], tt, gd[:, 256:512], OP.add))
+
+    rs = check(0, own)
+    tw = variables(0, rs, T.Tw)
+    need("G", tw)
+    send_raw(2, T.Tw)
+    need("P", ni[0], tw)
+    sg = [bank(T["bk%d" % (6 + i)], 0) for i in range(2)]
+    for i in range(2):
+        run("P", ten.matmul(sg[i], T.NI[:, :], bank(T.Rv0, diff[i]), True, False))
+    less_own((2, 3, RAW))
+    got = by_slots(2, T.Tw[:, 0:256], T.sn16, (T.Tg1, T.Lm1, T.Xm1, T.Dw1), [tw])
+    need("P", *got.values())
+    for i in range(2):
+        t = run("P", ten.matmul(sg[i], eye, bank(T.Tg1, diff[i]), False, True))
+        need("A", t)
+        sv[0] = run("A", act.activation(bank(T.sv1, i), sg[i], AF.Sign, bias=0.5))
+    gather_raw(2)
+    rs = check(1, got[0])
+    yt = variables(1, rs, T.ys)
+    need("S", yt)
+    g.sync.dma_start(T.y[:, :], T.ys[:, :]).then_inc(T.sem.dy, 16)
+    need("S", ("dy", 16))
+    for q in ("V", "A", "P", "G"):
+        need("G", ("s" + q, cnt[q]))
+    need("G", ("ls", cnt["ls"]))

@@ -5,18 +5,21 @@ NR, CAP, V, M = 8, 160, 256, 128
 W = NR * CAP
 BK = 2 * CAP
 H = 2 * BK
-NJ = 9 * M
+NJ = 8 * M
 NH = NJ // 2
+G1, G0 = 256, 384
 B = 51.0
+K = float(2 ** 20)
 OFF = 64
 OP = AluOpType
 AF = ActivationFunctionType
 RAW = 5
-TO_CHECKS = {"V": "g7 g4 g1 g0", "A": "g3 g2 g6 c4 c1", "recv": "V0 A5 V7 A3 V2 A6",
+TO_CHECKS = {"V": "g7 g4 g1 g0 c1", "A": "g3 g2 g6 c4", "recv": "V0 s0 A5 V7 A3 A2 V6",
              "calls": [[(5, 0, 8)], [(7, 0, 4), (3, 4, 4)], [(6, 0, 4), (2, 4, 4)], [(4, 0, 4), (1, 4, 4)]]}
-TO_VARS = {"V": "g7 g5 g4 g1 g0", "A": "g3 g2 g6 c5 c4 c1", "recv": "A0 V3 V7 V2 V6",
+PART = {"a": (0, 64), "b": (64, CAP)}
+TO_VARS = {"V": "a3 g7 g5 g4 g1 g0 c1", "A": "b3 g2 s1 g6 c5 c4", "recv": "A0 V3 V7 V2 V6",
            "calls": [[(3, 0, 8)], [(7, 0, 4), (2, 4, 4)], [(6, 0, 4), (5, 4, 4)], [(4, 0, 4), (1, 4, 4)]]}
-PLAN = {0: dict(TO_CHECKS, recv="V0 A7 A3 V5 V2 A6"), 1: TO_VARS, 2: TO_CHECKS, 3: TO_VARS}
+PLAN = {0: dict(TO_CHECKS, V="g7 g4 g1 x0 c1", A="g3 g2 g6 c4 g0", recv="A0 s0 A7 V3 V5 A2 V6"), 1: TO_VARS, 2: TO_CHECKS, 3: TO_VARS}
 
 SCRATCH = {
     "sn32": ("sbuf", [128, 80], "int32"), "pl32": ("sbuf", [128, 64], "int32"), "vl32": ("sbuf", [128, 64], "int32"),
@@ -26,12 +29,15 @@ SCRATCH = {
     "td": ("sbuf", [128, 64], "int32"), "pc16": ("sbuf", [128, 64], "uint16"),
     "num": ("sbuf", [128, 512], "float32"), "num2": ("sbuf", [128, 512], "float32"),
     "iva": ("sbuf", [128, W], "float32"), "ivb": ("sbuf", [128, W], "float32"),
-    "inv32": ("sbuf", [128, 80], "float32"), "inv16": ("sbuf", [128, 80], "uint16"),
-    "one": ("sbuf", [128, 256], "bfloat16"), "E": ("sbuf", [128, 256], "bfloat16"), "NI": ("sbuf", [128, 128], "bfloat16"),
+    "inva": ("sbuf", [128, 80], "float32"), "invb": ("sbuf", [128, 80], "float32"), "inv32": ("sbuf", [128, 80], "float32"),
+    "inv16": ("sbuf", [128, 80], "uint16"),
+    "one": ("sbuf", [128, 128], "bfloat16"), "E": ("sbuf", [128, 256], "bfloat16"), "NI": ("sbuf", [128, 128], "bfloat16"),
+    "EK": ("sbuf", [128, 256], "bfloat16"), "NK": ("sbuf", [128, 128], "bfloat16"),
     "xs": ("sbuf", [128, 256], "bfloat16"), "Tw": ("sbuf", [128, 256], "bfloat16"), "ys": ("sbuf", [128, 256], "float32"),
-    "D": ("sbuf", [128, NJ], "bfloat16"), "A": ("sbuf", [128, NJ], "bfloat16"), "NA": ("sbuf", [128, NJ], "bfloat16"),
-    "F": ("sbuf", [128, NJ], "bfloat16"), "Z": ("sbuf", [128, NH], "bfloat16"),
-    "C0": ("sbuf", [128, 2 * NJ], "bfloat16"), "C1": ("sbuf", [128, 2 * NJ], "bfloat16"), "C2": ("sbuf", [128, 2 * NJ], "bfloat16"),
+    "D": ("sbuf", [128, NJ], "bfloat16"), "A": ("sbuf", [128, NJ + 3], "bfloat16"), "F": ("sbuf", [128, NJ], "bfloat16"),
+    "Z": ("sbuf", [128, NH], "bfloat16"), "Zf": ("sbuf", [128, NH], "bfloat16"),
+    "Pre": ("sbuf", [128, NJ], "bfloat16"), "Suf": ("sbuf", [128, NJ], "bfloat16"),
+    "S": ("sbuf", [128, NJ], "bfloat16"), "U": ("sbuf", [128, NJ], "bfloat16"), "Rc": ("sbuf", [128, NJ], "bfloat16"),
     "sc": ("sbuf", [128, H], "bfloat16"), "so": ("sbuf", [128, H], "bfloat16"), "Rf": ("sbuf", [128, H], "bfloat16"),
 }
 for _d in range(NR):
@@ -40,7 +46,7 @@ for _r in range(2):
     for _n, _w in (("Tg", W), ("Rs", W), ("Lm", W), ("Lr", W), ("Xm", W), ("Xr", W), ("Dw", W), ("Rv", W), ("Gv", 1024), ("sv", H),
                    ("rx", 256)):
         SCRATCH["%s%d" % (_n, _r)] = ("sbuf", [128, _w], "bfloat16")
-SEMAPHORES = ["sV", "sA", "sP", "sG", "dx", "dsn", "dpl", "dvl", "df", "dr", "da", "dy", "ls", "rn"]
+SEMAPHORES = ["sV", "sA", "sP", "sG", "dx", "dsn", "dpl", "dvl", "df", "dr", "dy", "ls", "rn"]
 SEMAPHORES += ["arr%d_%d" % (ph, p) for ph in range(4) for p in range(NR)]
 
 
@@ -84,27 +90,37 @@ def rank_program(g, core, T, topo):
     def turn(ph, r):
         k = me * r if ph % 2 == 0 else -me * r
         s = (128 - 16 * (k % 8)) % 128
-        return T.E[:, s:s + 128]
-
-    def const(ap, n, value):
-        return run("G", g.iota(ap, [[0, n]], value, 0, allow_small_or_imprecise_dtypes=True))
+        return (T.EK if ph % 2 else T.E)[:, s:s + 128]
 
     eye = T.E[:, 0:128]
     g.sync.dma_start(T.sn32[:, :], T.sn[:, :]).then_inc(T.sem.dsn, 16)
     act.dma_start(T.xs[:, :], T.x[:, :]).then_inc(T.sem.dx, 16)
-    g.sync.dma_start(T.pl32[:, :], T.pl[:, :]).then_inc(T.sem.dpl, 16)
+    for u in range(8):
+        g.sync.dma_start(T.pl32[:, 8 * u:8 * u + 8], T.pl[u:128:8, :]).then_inc(T.sem.dpl, 16)
     act.dma_start(T.vl32[:, :], T.vl[:, :]).then_inc(T.sem.dvl, 16)
-    sn_in, x_in, pl_in, vl_in = ("dsn", 16), ("dx", 16), ("dpl", 16), ("dvl", 16)
-    num = run("G", g.iota(T.num[:, :], [[2, 4], [18, 128]], 1 + OFF, 0, allow_small_or_imprecise_dtypes=True))
+    sn_in, x_in, pl_in, vl_in = ("dsn", 16), ("dx", 16), ("dpl", 128), ("dvl", 16)
+    num = run("G", g.iota(T.num[:, 0:256], [[1, 256]], OFF, 0, allow_small_or_imprecise_dtypes=True))
     ones = run("V", vec.memset(T.one[:, :], 1.0))
     need("G", ones)
-    eyes = run("G", g.affine_select(T.E[:, :], T.one[:, :], [[0, 2], [-1, 128]], OP.is_equal, 0.0, 0, 1))
+    eye1 = run("G", g.affine_select(eye, T.one[:, :], [[-1, 128]], OP.is_equal, 0.0, 0, 1))
     need("A", ones)
-    run("A", act.activation(T.C1[:, 1:2 * NJ:NJ], T.one[:, 0:2], AF.Silu, bias=B - 1.0))
-    zero = run("V", vec.memset(T.Z[:, :], 0.0))
-    fill = run("V", vec.memset(T.iva[:, :], 0.0))
+    run("A", act.activation(T.A[:, 0:NJ + 3:NH + 1], T.one[:, 0:3], AF.Silu))
+    fill = run("V", vec.memset(T.inv32[:, :], 0.0))
     need("S", fill)
-    g.sync.dma_start(T.ivb[0:128:16, :], T.iva[0:128:16, :]).then_inc(T.sem.df, 16)
+    for win in (T.iva, T.ivb):
+        g.sync.dma_start(win[0:128:16, :], T.inv32[:, :]).then_inc(T.sem.df, 16)
+    z = [run("V", vec.memset(T.Zf[:, :], -1.0)), run("V", vec.memset(T.Z[:, :], 0.0))]
+    need("V", *z)
+    z = [run("V", vec.memset(T.Zf[:, 0:NH:8], 1.0)), run("V", vec.memset(T.Z[:, 0:NH:8], B / K))]
+    need("V", num)
+    num = run("V", vec.tensor_scalar(T.num[:, 256:512], T.num[:, 0:256], 256.0, None, OP.add))
+    need("A", num)
+    num2 = run("A", act.activation(T.num2[:, :], T.num[:, :], AF.Identity, bias=512.0))
+    need("V", eye1)
+    eyes = run("V", vec.tensor_copy(T.E[:, 128:256], eye))
+    ni = [run("V", vec.tensor_scalar(o[:, :], eye, s, None, OP.mult)) for o, s in ((T.NI, -1.0), (T.NK, -K))][-1]
+    need("V", eyes)
+    ek = run("V", vec.tensor_scalar(T.EK[:, :], T.E[:, :], K, None, OP.mult))
     need("V", sn_in)
     sn16 = run("V", vec.tensor_copy(T.sn16[:, :], T.sn32[:, :]))
 
@@ -134,8 +150,8 @@ def rank_program(g, core, T, topo):
     def drain(ph, q, out, src):
         if ph % 2 == 0:
             if q == "V":
-                return run("V", vec.tensor_scalar(out, src, 2.0, 1.0, OP.mult, OP.add))
-            return run("A", act.activation(out, src, AF.Identity, bias=1.0, scale=2.0))
+                return run("V", vec.tensor_scalar(out, src, 1.0 / 512, 1.0 / 1024, OP.mult, OP.add))
+            return run("A", act.activation(out, src, AF.Identity, bias=1.0 / 1024, scale=1.0 / 512))
         if q == "V":
             return run("V", vec.tensor_copy(out, src))
         return run("A", act.activation(out, src, AF.Copy))
@@ -146,41 +162,55 @@ def rank_program(g, core, T, topo):
         need("V", *ready)
         need("A", *ready)
 
-        def gather(q, d):
+        def gather(q, d, lo, hi):
             r = me ^ d
-            i, o = win.indirect(lst[:, r * CAP // 16:(r + 1) * CAP // 16]), blk(src, r)
+            i, o = win.indirect(lst[:, (r * CAP + lo) // 16:(r * CAP + hi) // 16]), src[:, r * CAP + lo:r * CAP + hi]
             if q == "A":
                 return run("A", act.activation(o, i, AF.Copy))
             if ph == 2 and not d & 2:
                 return run("V", vec.tensor_tensor(o, i, blk(T.Rv0, r), OP.subtract))
             if ph % 2 and not d & 2:
+                need("V", sc[d])
                 return run("V", vec.tensor_tensor(o, i, half(T.sc, r), OP.mult))
             return run("V", vec.tensor_copy(o, i))
 
         todo = {q: toks(ph, q) for q in "VA"}
         while todo["V"] or todo["A"]:
             for q in "VA":
-                while todo[q] and (todo[q][0][0] == "g" or todo[q][0][1] in trn):
+                while todo[q] and (todo[q][0][1] in trn if todo[q][0][0] == "c" else
+                                   q == "A" or ph % 2 == 0 or todo[q][0][1] & 2 or todo[q][0][1] in sc):
                     kind, d = todo[q].pop(0)
                     r = me ^ d
+                    if kind == "x":
+                        places()
+                        continue
+                    if kind == "s":
+                        own_sign(T["Dw%d" % (ph // 2)], d, arrived(ph - 1, d))
+                        continue
                     if kind == "c":
                         need(q, trn[d])
                         out[d] = drain(ph, q, blk(xsrc, r), ps(d))
                         continue
-                    got[d] = gather(q, d)
+                    if kind != "g":
+                        out.setdefault("first", []).append(gather(q, d, *PART[kind]))
+                    got[d] = gather(q, d, 0, CAP) if kind == "g" else out["first"][-1]
                     if d in xs:
-                        need("P", eyes, got[d])
+                        need("P", ek if ph % 2 else eyes, got[d])
                         trn[d] = run("P", ten.matmul(ps(d), turn(ph, r), blk(src, r), True, True))
         for c in PLAN[ph]["calls"][(ph + 1) % 2:]:
             for d, o, n in c:
-                need("G", out[d] if d in xs else got[d])
+                need("G", out[d] if d in xs else got[d], *out.get("first", []))
             send([(d, o, n, blk(xsrc if d in xs else src, me ^ d), blk(xland if d in xs else land, me), "arr%d_%d" % (ph, me))
                   for d, o, n in c])
         return got
 
+    def own_sign(dwin, d, there):
+        need("A", there)
+        sc[d] = run("A", act.activation(half(T.sc, me ^ d), blk(dwin, me ^ d), AF.Sign))
+
     def taken(ph, mine, mine_ready, land, rv, early=None):
         done, ev, left = {}, {}, [early] if early else []
-        for q, d in toks(ph, "recv"):
+        for q, d in [t for t in toks(ph, "recv") if t[0] != "s"]:
             p = me ^ d
             need("P", rawg[ph] if (ph, d) in ((0, RAW), (2, RAW)) else arrived(ph, d) if d else mine_ready)
             done[d] = run("P", ten.matmul(ps(d), turn(ph, p), blk(land if d else mine, p), not (ph == 2 and (d & 2 or d == RAW)), True))
@@ -188,6 +218,9 @@ def rank_program(g, core, T, topo):
                 left.pop()()
         for q, d in toks(ph, "recv"):
             p = me ^ d
+            if q == "s":
+                own_sign(rv, d, ev[d])
+                continue
             need(q, done[d])
             if ph % 2 and d & 2:
                 need("V", sv[0])
@@ -203,51 +236,48 @@ def rank_program(g, core, T, topo):
         win = T["rx%d" % (ph // 2)][:, 0:256]
         rawg[ph] = run("V", vec.tensor_copy(blk(T["Lm%d" % (ph // 2)], me ^ RAW), win.indirect(T.rn16[:, :])))
 
-    inv, rf, sv, ni, rawg = [None], [None], [None], [None], {}
+    def places():
+        need("V", pl_in)
+        ta = run("V", vec.tensor_scalar(T.ta[:, :], T.pl32[:, :], 15, None, OP.bitwise_and))
+        tb = run("V", vec.tensor_scalar(T.tb[:, :], T.pl32[:, :], 4, None, OP.arith_shift_right))
+        need("V", ta)
+        tc = run("V", vec.tensor_scalar(T.tc[:, :], T.ta[:, :], 80.0, None, OP.mult))
+        td.append(run("V", vec.tensor_copy(T.pl16[:, :], T.pl32[:, :])))
+        need("V", tb, tc)
+        td[0] = run("V", vec.tensor_tensor(T.td[:, :], T.tc[:, :], T.tb[:, :], OP.add))
+
+    inv, rf, sv, td, rawg, sc = [None], [None], [None], [None], {}, {}
     need("G", x_in)
     send_raw(0, T.xs)
     need("G", sn_in)
     send([(RAW, 0, 8, T.sn32[:, (me ^ RAW) * 10:(me ^ RAW) * 10 + 10], T.rn32[:, :], "rn")])
     own = by_slots(0, T.xs[:, 0:256], T.sn16, (T.Tg0, T.Lm0, T.Xm0, T.Dw0), [sn16, x_in])[0]
-    need("A", num)
-    num2 = run("A", act.activation(T.num2[:, :], T.num[:, :], AF.Silu, bias=8.0))
-    need("V", pl_in)
-    ta = run("V", vec.tensor_scalar(T.ta[:, :], T.pl32[:, :], 15, None, OP.bitwise_and))
-    tb = run("V", vec.tensor_scalar(T.tb[:, :], T.pl32[:, :], 4, None, OP.arith_shift_right))
-    need("V", ta)
-    tc = run("V", vec.tensor_scalar(T.tc[:, :], T.ta[:, :], 80.0, None, OP.mult))
-    pl16 = run("V", vec.tensor_copy(T.pl16[:, :], T.pl32[:, :]))
-    need("V", tb, tc)
-    td = run("V", vec.tensor_tensor(T.td[:, :], T.tc[:, :], T.tb[:, :], OP.add))
+    pl16 = td[1]
+    need("V", td[0])
+    pc = run("V", vec.tensor_copy(T.pc16[:, :], T.td[:, :]))
     need("V", vl_in)
     vl16 = run("V", vec.tensor_copy(T.vl16[:, :], T.vl32[:, :]))
-    need("V", td)
-    pc = run("V", vec.tensor_copy(T.pc16[:, :], T.td[:, :]))
-    need("V", pc, fill, num, ("df", 16))
+    need("V", pc, num, ("df", 32))
     scat = run("V", vec.tensor_copy(T.iva[:, 0:W].indirect(T.pc16[:, 0:32]), T.num[:, :]))
-    need("A", pc, num2, ("df", 16))
+    need("A", pc, num2, ("df", 32))
     scat2 = run("A", act.activation(T.ivb[:, 0:W].indirect(T.pc16[:, 32:64]), T.num2[:, :], AF.Silu))
     need("S", scat)
-    g.sync.dma_start(T.inv32[:, :], T.iva[0:128:16, :]).then_inc(T.sem.dr, 16)
+    g.sync.dma_start(T.inva[:, :], T.iva[0:128:16, :]).then_inc(T.sem.dr, 16)
+    need("S", scat2)
+    g.sync.dma_start(T.invb[:, :], T.ivb[0:128:16, :]).then_inc(T.sem.dr, 16)
     need("V", ("rn", 8))
     rn16 = run("V", vec.tensor_copy(T.rn16[:, :], T.rn32[:, :]))
     need("V", rn16)
     gather_raw(0)
-    need("G", zero)
-    const(T.Z[:, 8:NH:9], M // 2, int(B))
-    const(T.D[:, 8:NJ:9], M, 0)
-    z = const(T.C1[:, NJ - 2:2 * NJ:NJ], 2, 0)
-    c0 = {k: const(T.C0[:, k * NJ:(k + 1) * NJ:2], NH, 64) for k in (1, 0)}
-    need("G", scat2, ("dr", 16))
-    g.dma_start(T.inv32[:, :], T.ivb[0:128:16, :], accum_op=OP.add).then_inc(T.sem.da, 16)
 
     def less_own(ds):
-        need("P", ni[0], rf[0])
+        need("P", ni, rf[0])
         for d in ds:
-            run("P", ten.matmul(ps(d), T.NI[:, :], half(T.Rf, me ^ d) if d & 2 else blk(T.Rs0, me ^ d), True, False))
+            run("P", ten.matmul(ps(d), T.NK[:, :], half(T.Rf, me ^ d) if d & 2 else blk(T.Rs0, me ^ d), True, False))
 
     def check(r, mine_ready):
         dwin = T["Dw%d" % r]
+        sc.clear()
 
         def late():
             need("P", sv[0])
@@ -257,89 +287,89 @@ def rank_program(g, core, T, topo):
         win = dwin[:, 0:W]
         need("V", pl16, *ev.values())
         need("A", pl16, *ev.values())
-        for e in range(4):
-            gv = run("V", vec.tensor_copy(T.D[:, e:NJ:9], win.indirect(T.pl16[:, 8 * e:8 * e + 8])))
-            ga = run("A", act.activation(T.D[:, e + 4:NJ:9], win.indirect(T.pl16[:, 8 * e + 32:8 * e + 40]), AF.Copy))
-        need("V", gv, ga, z)
-        need("A", gv, ga, z)
+        need("V", *z)
 
         def part(buf, k):
             return buf[:, k * NH:(k + 1) * NH]
 
-        ab, na, lim, neg, suf, w, fs, f, pre = {}, {}, {}, {}, {}, {}, {}, {}, {}
-        for k in (1, 0):
-            f[k] = run("V", vec.tensor_tensor_scan(part(T.F, k), part(T.D, k), T.Z[:, :], B, OP.mult, OP.add))
-            ab[k] = run("A", act.activation(part(T.A, k), part(T.D, k), AF.Abs, bias=-0.5, scale=0.5))
+        edges, ab, f, sg, pre, suf, u, w = {0: [], 1: []}, {}, {}, {}, {}, {}, {}, {}
+        at = [1, NH + 2]
+
+        def fetch(q, lo, hi):
+            o, i = T.D[:, lo:hi], win.indirect(T.pl16[:, lo // 16:hi // 16])
+            edges[lo // NH].append(run("V", vec.tensor_copy(o, i)) if q == "V" else run("A", act.activation(o, i, AF.Copy)))
+
+        def sizes(k):
+            need("A", *edges[k])
+            ab[k] = run("A", act.activation(T.A[:, at[k]:at[k] + NH], part(T.D, k), AF.Abs, bias=-0.5 / K, scale=512 / K))
+
+        def product(k):
+            need("V", *edges[k])
+            f[k] = run("V", vec.tensor_tensor_scan(part(T.F, k), T.Zf[:, :], part(T.D, k), 0.0, OP.max, OP.mult))
+
+        def sign(k):
+            need("P", f[k])
+            for e in range(8):
+                t = run("P", ten.matmul(T["bk%d" % (2 + k)][:, e:NH:8], eye, T.F[:, k * NH + 7:(k + 1) * NH:8], True, True))
+            need("A", t)
+            sg[k] = run("A", act.activation(part(T.S, k), T["bk%d" % (2 + k)][:, :], AF.Sign))
 
         def before(k):
             need("V", ab[k])
-            lo, hi = k * NH + 1, (k + 1) * NH
-            pre[k] = run("V", vec.tensor_tensor_scan(T.C1[:, 2 * lo + 1:2 * hi:2], T.A[:, lo - 1:hi - 1], T.Z[:, :NH - 1], B, OP.min, OP.max))
-
-        def negative(k):
-            lo, hi = k * NH + 1, (k + 1) * NH
-            need("A", pre[k], c0[k])
-            neg[k] = run("A", act.activation(T.C0[:, 2 * lo - 1:2 * hi:2], T.C1[:, 2 * lo - 1:2 * hi:2], AF.Copy, scale=-1.0))
-
-        def negate(k):
-            if k:
-                need("V", ab[k])
-                na[k] = run("V", vec.tensor_scalar(part(T.NA, k), part(T.A, k), -1.0, None, OP.mult))
-            else:
-                need("A", ab[k])
-                na[k] = run("A", act.activation(part(T.NA, k), part(T.A, k), AF.Copy, scale=-1.0))
-
-        def limit(k):
-            need("G", na[k])
-            lim[k] = const(T.NA[:, k * NH + 8:(k + 1) * NH:9], M // 2, 64)
-
-        def start(k):
-            lo, hi = k * NH, (k + 1) * NH
-            need("V", f[k], na[k], pre[k])
-            fs[k] = run("V", vec.tensor_copy(T.A[:, lo + 8:hi:9], T.F[:, lo + 7:hi:9]))
+            pre[k] = run("V", vec.tensor_tensor_scan(part(T.Pre, k), T.A[:, at[k] - 1:at[k] + NH - 1], T.Z[:, :], 0.0, OP.min, OP.max))
 
         def behind(k):
-            need("V", fs[k], lim[k])
-            top = (k + 1) * NH - 1
-            cols, to = slice(top, k * NH, -1), slice(2 * (top - 1), 2 * k * NH - 2 if k else None, -2)
-            suf[k] = run("V", vec.tensor_tensor_scan(T.C1[:, to], T.NA[:, cols], T.A[:, cols], 0.0, OP.max, OP.min))
+            need("V", ab[k])
+            suf[k] = run("V", vec.tensor_tensor_scan(T.Suf[:, NJ - 1:NH - 1:-1] if k else T.Suf[:, NH - 1::-1], T.A[:, at[k] + NH:at[k]:-1],
+                                                     T.Z[:, :], 0.0, OP.min, OP.max))
 
-        def both(k):
-            need("V", suf[k], neg[k])
-            c = slice(2 * k * NH, 2 * (k + 1) * NH)
-            w[k] = run("V", vec.tensor_tensor_scan(T.C2[:, c], T.C0[:, c], T.C1[:, c], 0.0, OP.max, OP.min))
+        def first(k):
+            need("V", pre[k], suf[k])
+            pre[k] = run("V", vec.tensor_copy(T.Pre[:, k * NH:(k + 1) * NH:8], T.Suf[:, k * NH:(k + 1) * NH:8]))
 
-        negate(0)
-        negate(1)
-        before(1)
-        limit(1)
-        negative(1)
-        before(0)
-        limit(0)
-        negative(0)
-        start(1)
-        behind(1)
-        start(0)
-        behind(0)
-        both(1)
+        def both(lo, hi):
+            need("V", pre[lo // NH])
+            u[lo] = run("V", vec.tensor_tensor_scan(T.U[:, lo:hi], T.Suf[:, lo:hi], T.Pre[:, lo:hi], 0.0, OP.max, OP.min))
+
+        def signed(lo, hi):
+            need("V", u[lo], sg[lo // NH])
+            w[lo] = run("V", vec.tensor_tensor_scan(T.Rc[:, lo:hi], T.S[:, lo:hi], T.U[:, lo:hi], 0.0, OP.add, OP.mult))
+
+        fetch("V", NH, NH + G1)
+        fetch("A", NH + G1, NJ)
+        fetch("V", 0, G0)
+        sizes(1)
+        fetch("A", G0, NH)
+        sizes(0)
+        product(1)
+        sign(1)
+        for step, k in ((before, 1), (behind, 1), (product, 0), (sign, 0), (first, 1), (before, 0), (behind, 0)):
+            step(k)
+        for d in (RAW, 4):
+            own_sign(dwin, d, ev[d])
+        both(NH, NJ)
+        first(0)
+        signed(NH, NJ)
         if r == 0:
-            need("V", ("da", 16))
+            need("V", ("dr", 32))
+            inv[0] = run("V", vec.tensor_tensor(T.inv32[:, :], T.inva[:, :], T.invb[:, :], OP.add))
+        both(0, NH // 2)
+        both(NH // 2, NH)
+        if r == 0:
+            need("V", inv[0])
             inv[0] = run("V", vec.tensor_scalar(T.inv16[:, :], T.inv32[:, :], 0.25 - OFF, 0.0, OP.add, OP.max))
-        both(0)
-        for i in range(2):
-            sc = run("A", act.activation(bank(T.sc, i), bank(dwin, same[i]), AF.Sign))
+        signed(0, NH // 2)
+        signed(NH // 2, NH)
         dst = T["Rs%d" % r]
-        got = by_slots(2 * r + 1, T.C2[:, 0:2 * NJ], T.inv16, (dst, T["Lr%d" % r], T["Xr%d" % r], T["Rv%d" % r]), [w[1], w[0], inv[0], sc])
+        got = by_slots(2 * r + 1, T.Rc[:, 0:NJ], T.inv16, (dst, T["Lr%d" % r], T["Xr%d" % r], T["Rv%d" % r]), [*w.values(), inv[0]])
         if r == 0:
             for i in range(2):
                 so = run("A", act.activation(bank(T.so, i), bank(dwin, diff[i]), AF.Sign))
             for i in range(2):
                 sv[0] = run("A", act.activation(bank(T.sv0, i), bank(T.Tg0, diff[i]), AF.Sign, bias=0.5))
-            need("A", eyes)
-            ni[0] = run("A", act.activation(T.NI[:, :], eye, AF.Copy, scale=-1.0))
             need("V", so, *got.values())
             for i in range(2):
-                rf[0] = run("V", vec.tensor_tensor(bank(T.Rf, i), bank(dst, diff[i]), bank(T.so, i), OP.mult))
+                rf[0] = run("V", vec.tensor_tensor_scan(bank(T.Rf, i), bank(T.so, i), bank(dst, diff[i]), 0.0, OP.add, OP.mult))
         return got[0]
 
     def variables(r, rs, out):
@@ -372,7 +402,7 @@ def rank_program(g, core, T, topo):
     tw = variables(0, rs, T.Tw)
     need("G", tw)
     send_raw(2, T.Tw)
-    need("P", ni[0], tw)
+    need("P", ni, tw)
     sg = [bank(T["bk%d" % (6 + i)], 0) for i in range(2)]
     for i in range(2):
         run("P", ten.matmul(sg[i], T.NI[:, :], bank(T.Rv0, diff[i]), True, False))

@@ -7,34 +7,50 @@ BK = 2 * CAP
 H = 2 * BK
 NJ = 8 * M
 NH = NJ // 2
-G1, G0 = 256, 384
+PC = 256
+VA = 192
 B = 51.0
 K = float(2 ** 20)
 OFF = 64
 OP = AluOpType
 AF = ActivationFunctionType
 RAW = 5
-TO_CHECKS = {"V": "g7 g4 g1 g0 c1", "A": "g3 g2 g6 c4", "recv": "V0 s0 A5 V7 A3 A2 V6",
+TO_CHECKS = {"V": "g7 g4 g1 g0 c1", "A": "g3 g2 g6 c4", "recv": "V0 s0 A5 s5 V7 A3 A2 V6",
              "calls": [[(5, 0, 8)], [(7, 0, 4), (3, 4, 4)], [(6, 0, 4), (2, 4, 4)], [(4, 0, 4), (1, 4, 4)]]}
 PART = {"a": (0, 64), "b": (64, CAP)}
-TO_VARS = {"V": "a3 g7 g5 g4 g1 g0 c1", "A": "b3 g2 s1 g6 c5 c4", "recv": "A0 V3 V7 V2 V6",
-           "calls": [[(3, 0, 8)], [(7, 0, 4), (2, 4, 4)], [(6, 0, 4), (5, 4, 4)], [(4, 0, 4), (1, 4, 4)]]}
-PLAN = {0: dict(TO_CHECKS, V="g7 g4 g1 x0 c1", A="g3 g2 g6 c4 g0", recv="A0 s0 A7 V3 V5 A2 V6"), 1: TO_VARS, 2: TO_CHECKS, 3: TO_VARS}
+TO_VARS = {"V": "a3 g5 g4 g1 g0 c1", "A": "b3 g7 g2 g6 c4", "recv": "A0 V3 V7 A5 V2 V6",
+           "calls": [[(3, 0, 8)], [(7, 0, 4), (5, 4, 4)], [(2, 0, 4), (6, 4, 4)], [(4, 0, 4), (1, 4, 4)]]}
+LIST = (0, 8)
+FIRST = dict(TO_CHECKS, V="a5 g7 x0 g4 x1 g1 x2 c4 x3 c1", A="b5 g3 g2 g6 g0 n0", recv="A5 V0 V7 A3 V2 A6")
+SV = 512
+PLAN = {0: FIRST, 1: dict(TO_VARS, A="b3 g7 g2 s0 g6 c4"), 2: TO_CHECKS, 3: TO_VARS}
+READS = {"edges": [], "size": ["edges"], "product": ["edges"], "repeat": ["product"], "sign": ["repeat"], "before": ["size"],
+         "behind": ["size"], "first": ["before", "behind"], "least": ["first"], "signed": ["least", "sign"]}
+
+
+H0, H1 = (0, NH), (NH, NJ)
+Q0, Q1, Q2, Q3 = [(a, a + PC) for a in range(0, NJ, PC)]
+CHECK = {"V": [("edges", *Q0), ("edges", 512, 640), ("product", *H0), ("edges", 640, 768), ("before", *Q0), ("behind", *Q0), ("product", *H1)]
+         + [(n, *q) for q in (Q1, Q2, Q3) for n in ("before", "behind")]
+         + [("least", *H0), ("least", *Q2), ("least", *Q3), ("list", 0, 0), ("signed", *H0), ("signed", *H1)],
+         "A": [("edges", *Q1), ("edges", 768, 864), ("size", *Q0), ("edges", 864, NJ), ("size", *Q1), ("size", *Q2), ("size", *Q3),
+               ("sign", *Q0), ("first", *H0), ("sign", *Q1), ("first", *Q2), ("first", *Q3), ("sign", *H1)],
+         "P": [("repeat", *H0), ("repeat", *H1), ("list", 0, 0)]}
 
 SCRATCH = {
     "sn32": ("sbuf", [128, 80], "int32"), "pl32": ("sbuf", [128, 64], "int32"), "vl32": ("sbuf", [128, 64], "int32"),
     "sn16": ("sbuf", [128, 80], "uint16"), "pl16": ("sbuf", [128, 64], "uint16"), "vl16": ("sbuf", [128, 64], "uint16"),
-    "rn32": ("sbuf", [128, 10], "int32"), "rn16": ("sbuf", [128, 10], "uint16"),
+    "pm32": ("sbuf", [128, 64], "int32"), "ln32": ("sbuf", [128, 10], "int32"), "rn32": ("sbuf", [128, 10], "int32"), "rn16": ("sbuf", [128, 10], "uint16"),
     "ta": ("sbuf", [128, 64], "int32"), "tb": ("sbuf", [128, 64], "int32"), "tc": ("sbuf", [128, 64], "int32"),
     "td": ("sbuf", [128, 64], "int32"), "pc16": ("sbuf", [128, 64], "uint16"),
-    "num": ("sbuf", [128, 512], "float32"), "num2": ("sbuf", [128, 512], "float32"),
+    "num": ("sbuf", [128, NJ], "float32"),
     "iva": ("sbuf", [128, W], "float32"), "ivb": ("sbuf", [128, W], "float32"),
-    "inva": ("sbuf", [128, 80], "float32"), "invb": ("sbuf", [128, 80], "float32"), "inv32": ("sbuf", [128, 80], "float32"),
+    "inva": ("sbuf", [128, 80], "float32"), "invb": ("sbuf", [128, 80], "float32"), "nil": ("sbuf", [128, 320], "float32"),
     "inv16": ("sbuf", [128, 80], "uint16"),
     "one": ("sbuf", [128, 128], "bfloat16"), "E": ("sbuf", [128, 256], "bfloat16"), "NI": ("sbuf", [128, 128], "bfloat16"),
     "EK": ("sbuf", [128, 256], "bfloat16"), "NK": ("sbuf", [128, 128], "bfloat16"),
-    "xs": ("sbuf", [128, 256], "bfloat16"), "Tw": ("sbuf", [128, 256], "bfloat16"), "ys": ("sbuf", [128, 256], "float32"),
-    "D": ("sbuf", [128, NJ], "bfloat16"), "A": ("sbuf", [128, NJ + 3], "bfloat16"), "F": ("sbuf", [128, NJ], "bfloat16"),
+    "xs": ("sbuf", [128, 256], "bfloat16"), "Tw": ("sbuf", [128, 256], "bfloat16"), "E32": ("sbuf", [128, 128], "float32"), "ys": ("sbuf", [128, 256], "float32"),
+    "D": ("sbuf", [128, NJ], "bfloat16"), "A": ("sbuf", [128, NJ + NJ // PC + 1], "bfloat16"), "F": ("sbuf", [128, NJ], "bfloat16"),
     "Z": ("sbuf", [128, NH], "bfloat16"), "Zf": ("sbuf", [128, NH], "bfloat16"),
     "Pre": ("sbuf", [128, NJ], "bfloat16"), "Suf": ("sbuf", [128, NJ], "bfloat16"),
     "S": ("sbuf", [128, NJ], "bfloat16"), "U": ("sbuf", [128, NJ], "bfloat16"), "Rc": ("sbuf", [128, NJ], "bfloat16"),
@@ -46,7 +62,7 @@ for _r in range(2):
     for _n, _w in (("Tg", W), ("Rs", W), ("Lm", W), ("Lr", W), ("Xm", W), ("Xr", W), ("Dw", W), ("Rv", W), ("Gv", 1024), ("sv", H),
                    ("rx", 256)):
         SCRATCH["%s%d" % (_n, _r)] = ("sbuf", [128, _w], "bfloat16")
-SEMAPHORES = ["sV", "sA", "sP", "sG", "dx", "dsn", "dpl", "dvl", "df", "dr", "dy", "ls", "rn"]
+SEMAPHORES = ["sV", "sA", "sP", "sG", "dl", "dx", "dpm", "dsn", "dpl", "dvl", "df", "dr", "dy", "ls", "rn"]
 SEMAPHORES += ["arr%d_%d" % (ph, p) for ph in range(4) for p in range(NR)]
 
 
@@ -92,35 +108,44 @@ def rank_program(g, core, T, topo):
         s = (128 - 16 * (k % 8)) % 128
         return (T.EK if ph % 2 else T.E)[:, s:s + 128]
 
-    eye = T.E[:, 0:128]
+    def places(i):
+        need("V", pc[0] or pl_in)
+        if i == 0:
+            run("V", vec.tensor_scalar(T.ta[:, :], T.pl32[:, :], 15, None, OP.bitwise_and))
+            pc[0] = run("V", vec.tensor_scalar(T.tb[:, :], T.pl32[:, :], 4, None, OP.arith_shift_right))
+        elif i == 1:
+            pc[0] = run("V", vec.tensor_scalar(T.tc[:, :], T.ta[:, :], 80.0, None, OP.mult))
+        elif i == 2:
+            pc[0] = run("V", vec.tensor_tensor(T.td[:, :], T.tc[:, :], T.tb[:, :], OP.add))
+        else:
+            pc[0] = run("V", vec.tensor_copy(T.pc16[:, :], T.td[:, :]))
+
+    eye, pc = T.E[:, 0:128], [None]
+    act.dma_start(T.ln32[:, :], T.sn[:, (me ^ RAW) * 10:(me ^ RAW) * 10 + 10]).then_inc(T.sem.dl, 16)
     g.sync.dma_start(T.sn32[:, :], T.sn[:, :]).then_inc(T.sem.dsn, 16)
-    act.dma_start(T.xs[:, :], T.x[:, :]).then_inc(T.sem.dx, 16)
-    for u in range(8):
-        g.sync.dma_start(T.pl32[:, 8 * u:8 * u + 8], T.pl[u:128:8, :]).then_inc(T.sem.dpl, 16)
-    act.dma_start(T.vl32[:, :], T.vl[:, :]).then_inc(T.sem.dvl, 16)
-    sn_in, x_in, pl_in, vl_in = ("dsn", 16), ("dx", 16), ("dpl", 128), ("dvl", 16)
-    num = run("G", g.iota(T.num[:, 0:256], [[1, 256]], OFF, 0, allow_small_or_imprecise_dtypes=True))
+    g.sync.dma_start(T.xs[:, 0:256], T.x[:, :]).then_inc(T.sem.dx, 16)
+    g.sync.dma_start(T.pl32[:, :], T.pl[:, :]).then_inc(T.sem.dpl, 16)
+    sn_in, x_in, pl_in, pm_in, vl_in = ("dsn", 16), ("dx", 16), ("dpl", 16), ("dpm", 128), ("dvl", 16)
+    num = run("G", g.iota(T.num[:, 0:256], [[1, 2], [8, 16], [128, 8]], OFF, 0, allow_small_or_imprecise_dtypes=True))
     ones = run("V", vec.memset(T.one[:, :], 1.0))
     need("G", ones)
     eye1 = run("G", g.affine_select(eye, T.one[:, :], [[-1, 128]], OP.is_equal, 0.0, 0, 1))
     need("A", ones)
-    run("A", act.activation(T.A[:, 0:NJ + 3:NH + 1], T.one[:, 0:3], AF.Silu))
-    fill = run("V", vec.memset(T.inv32[:, :], 0.0))
+    run("A", act.activation(T.A[:, 0::PC + 1], T.one[:, 0:NJ // PC + 1], AF.Silu))
+    fill = run("V", vec.memset(T.nil[:, :], 0.0))
     need("S", fill)
     for win in (T.iva, T.ivb):
-        g.sync.dma_start(win[0:128:16, :], T.inv32[:, :]).then_inc(T.sem.df, 16)
+        g.sync.dma_start(win[0:128:16, :], T.nil[0:32, :]).then_inc(T.sem.df, 16)
+    for u in range(8):
+        g.sync.dma_start(T.pm32[:, 8 * u:8 * u + 8], T.pl[u:128:8, :]).then_inc(T.sem.dpm, 16)
     z = [run("V", vec.memset(T.Zf[:, :], -1.0)), run("V", vec.memset(T.Z[:, :], 0.0))]
+    need("V", num)
+    num = run("V", vec.tensor_scalar(T.num[:, 256:512], T.num[:, 0:256], 2.0, None, OP.add))
     need("V", *z)
     z = [run("V", vec.memset(T.Zf[:, 0:NH:8], 1.0)), run("V", vec.memset(T.Z[:, 0:NH:8], B / K))]
-    need("V", num)
-    num = run("V", vec.tensor_scalar(T.num[:, 256:512], T.num[:, 0:256], 256.0, None, OP.add))
-    need("A", num)
-    num2 = run("A", act.activation(T.num2[:, :], T.num[:, :], AF.Identity, bias=512.0))
     need("V", eye1)
     eyes = run("V", vec.tensor_copy(T.E[:, 128:256], eye))
-    ni = [run("V", vec.tensor_scalar(o[:, :], eye, s, None, OP.mult)) for o, s in ((T.NI, -1.0), (T.NK, -K))][-1]
-    need("V", eyes)
-    ek = run("V", vec.tensor_scalar(T.EK[:, :], T.E[:, :], K, None, OP.mult))
+    num2 = run("V", vec.tensor_scalar(T.num[:, 512:768], T.num[:, 0:256], 4.0, None, OP.add))
     need("V", sn_in)
     sn16 = run("V", vec.tensor_copy(T.sn16[:, :], T.sn32[:, :]))
 
@@ -181,11 +206,15 @@ def rank_program(g, core, T, topo):
                                    q == "A" or ph % 2 == 0 or todo[q][0][1] & 2 or todo[q][0][1] in sc):
                     kind, d = todo[q].pop(0)
                     r = me ^ d
+                    if kind == "n":
+                        need("A", num)
+                        late["num"] = run("A", act.activation(T.num[:, 768:NJ], T.num[:, 256:512], AF.Identity, bias=4.0))
+                        continue
                     if kind == "x":
-                        places()
+                        places(d)
                         continue
                     if kind == "s":
-                        own_sign(T["Dw%d" % (ph // 2)], d, arrived(ph - 1, d))
+                        own_sign(T["Dw%d" % (ph // 2)], d, late["ev"][d])
                         continue
                     if kind == "c":
                         need(q, trn[d])
@@ -195,9 +224,9 @@ def rank_program(g, core, T, topo):
                         out.setdefault("first", []).append(gather(q, d, *PART[kind]))
                     got[d] = gather(q, d, 0, CAP) if kind == "g" else out["first"][-1]
                     if d in xs:
-                        need("P", ek if ph % 2 else eyes, got[d])
+                        need("P", late["EK"] if ph % 2 else eyes, got[d])
                         trn[d] = run("P", ten.matmul(ps(d), turn(ph, r), blk(src, r), True, True))
-        for c in PLAN[ph]["calls"][(ph + 1) % 2:]:
+        for c in PLAN[ph]["calls"][int(ph == 2):]:
             for d, o, n in c:
                 need("G", out[d] if d in xs else got[d], *out.get("first", []))
             send([(d, o, n, blk(xsrc if d in xs else src, me ^ d), blk(xland if d in xs else land, me), "arr%d_%d" % (ph, me))
@@ -208,14 +237,12 @@ def rank_program(g, core, T, topo):
         need("A", there)
         sc[d] = run("A", act.activation(half(T.sc, me ^ d), blk(dwin, me ^ d), AF.Sign))
 
-    def taken(ph, mine, mine_ready, land, rv, early=None):
-        done, ev, left = {}, {}, [early] if early else []
+    def taken(ph, mine, mine_ready, land, rv):
+        done, ev = {}, {}
         for q, d in [t for t in toks(ph, "recv") if t[0] != "s"]:
             p = me ^ d
-            need("P", rawg[ph] if (ph, d) in ((0, RAW), (2, RAW)) else arrived(ph, d) if d else mine_ready)
+            need("P", rawg[ph] if (ph, d) == (2, RAW) else arrived(ph, d) if d else mine_ready)
             done[d] = run("P", ten.matmul(ps(d), turn(ph, p), blk(land if d else mine, p), not (ph == 2 and (d & 2 or d == RAW)), True))
-            if left:
-                left.pop()()
         for q, d in toks(ph, "recv"):
             p = me ^ d
             if q == "s":
@@ -232,141 +259,117 @@ def rank_program(g, core, T, topo):
         return ev
 
     def gather_raw(ph):
-        need("V", arrived(ph, RAW))
+        need("V", late["rn"], arrived(ph, RAW))
         win = T["rx%d" % (ph // 2)][:, 0:256]
         rawg[ph] = run("V", vec.tensor_copy(blk(T["Lm%d" % (ph // 2)], me ^ RAW), win.indirect(T.rn16[:, :])))
 
-    def places():
-        need("V", pl_in)
-        ta = run("V", vec.tensor_scalar(T.ta[:, :], T.pl32[:, :], 15, None, OP.bitwise_and))
-        tb = run("V", vec.tensor_scalar(T.tb[:, :], T.pl32[:, :], 4, None, OP.arith_shift_right))
-        need("V", ta)
-        tc = run("V", vec.tensor_scalar(T.tc[:, :], T.ta[:, :], 80.0, None, OP.mult))
-        td.append(run("V", vec.tensor_copy(T.pl16[:, :], T.pl32[:, :])))
-        need("V", tb, tc)
-        td[0] = run("V", vec.tensor_tensor(T.td[:, :], T.tc[:, :], T.tb[:, :], OP.add))
-
-    inv, rf, sv, td, rawg, sc = [None], [None], [None], [None], {}, {}
-    need("G", x_in)
-    send_raw(0, T.xs)
-    need("G", sn_in)
-    send([(RAW, 0, 8, T.sn32[:, (me ^ RAW) * 10:(me ^ RAW) * 10 + 10], T.rn32[:, :], "rn")])
+    inv, rf, sv, rawg, sc, late = [None], [None], [None], {}, {}, {}
+    need("G", ("dl", 16))
+    send([(RAW, *LIST, T.ln32[:, :], T.rn32[:, :], "rn")])
     own = by_slots(0, T.xs[:, 0:256], T.sn16, (T.Tg0, T.Lm0, T.Xm0, T.Dw0), [sn16, x_in])[0]
-    pl16 = td[1]
-    need("V", td[0])
-    pc = run("V", vec.tensor_copy(T.pc16[:, :], T.td[:, :]))
-    need("V", vl_in)
-    vl16 = run("V", vec.tensor_copy(T.vl16[:, :], T.vl32[:, :]))
-    need("V", pc, num, ("df", 32))
-    scat = run("V", vec.tensor_copy(T.iva[:, 0:W].indirect(T.pc16[:, 0:32]), T.num[:, :]))
-    need("A", pc, num2, ("df", 32))
-    scat2 = run("A", act.activation(T.ivb[:, 0:W].indirect(T.pc16[:, 32:64]), T.num2[:, :], AF.Silu))
+    need("V", pc[0], num2, ("df", 32))
+    scat = run("V", vec.tensor_copy(T.iva[:, 0:W].indirect(T.pc16[:, 0:SV // 16]), T.num[:, 0:SV]))
+    need("G", fill)
+    for o, n, s in ((T.E32, 1, 1.0), (T.EK, 2, K), (T.NI, 1, -1.0), (T.NK, 1, -K)):
+        late[o.name] = run("G", g.affine_select(o[:, :], T.nil[:, 0:128 * n], [[0, n], [-1, 128]], OP.not_equal, s, 0, 1))
+    need("A", pc[0], num2, late["num"], ("df", 32))
+    scat2 = run("A", act.activation(T.ivb[:, 0:W].indirect(T.pc16[:, SV // 16:64]), T.num[:, SV:NJ], AF.Silu))
     need("S", scat)
     g.sync.dma_start(T.inva[:, :], T.iva[0:128:16, :]).then_inc(T.sem.dr, 16)
     need("S", scat2)
     g.sync.dma_start(T.invb[:, :], T.ivb[0:128:16, :]).then_inc(T.sem.dr, 16)
-    need("V", ("rn", 8))
-    rn16 = run("V", vec.tensor_copy(T.rn16[:, :], T.rn32[:, :]))
-    need("V", rn16)
-    gather_raw(0)
+    g.sync.dma_start(T.vl32[:, :], T.vl[:, :]).then_inc(T.sem.dvl, 16)
+    need("V", pm_in)
+    pl16 = run("V", vec.tensor_copy(T.pl16[:, :], T.pm32[:, :]))
 
     def less_own(ds):
-        need("P", ni, rf[0])
+        need("P", late["NK"], rf[0])
         for d in ds:
             run("P", ten.matmul(ps(d), T.NK[:, :], half(T.Rf, me ^ d) if d & 2 else blk(T.Rs0, me ^ d), True, False))
 
     def check(r, mine_ready):
         dwin = T["Dw%d" % r]
         sc.clear()
-
-        def late():
-            need("P", sv[0])
-            less_own((6, 7))
-
-        ev = taken(2 * r, T["Tg%d" % r], mine_ready, T["Lm%d" % r], dwin, late if r else None)
+        ev = late["ev"] = taken(2 * r, T["Tg%d" % r], mine_ready, T["Lm%d" % r], dwin)
         win = dwin[:, 0:W]
         need("V", pl16, *ev.values())
         need("A", pl16, *ev.values())
         need("V", *z)
 
-        def part(buf, k):
-            return buf[:, k * NH:(k + 1) * NH]
+        made = {n: [] for n in READS}
 
-        edges, ab, f, sg, pre, suf, u, w = {0: [], 1: []}, {}, {}, {}, {}, {}, {}, {}
-        at = [1, NH + 2]
+        def one(q, name, lo, hi):
+            c, n, a = slice(lo, hi), hi - lo, 1 + lo + lo // PC
+            rep = T["bk%d" % (2 + lo // NH)]
+            if name == "edges":
+                o, i = T.D[:, c], win.indirect(T.pl16[:, lo // 16:hi // 16])
+                return vec.tensor_copy(o, i) if q == "V" else act.activation(o, i, AF.Copy)
+            if name == "size":
+                return act.activation(T.A[:, a:a + n], T.D[:, c], AF.Abs, bias=-0.5 / K, scale=512 / K)
+            if name == "product":
+                return vec.tensor_tensor_scan(T.F[:, c], T.Zf[:, 0:n], T.D[:, c], 0.0, OP.max, OP.mult)
+            if name == "repeat":
+                for e in range(7):
+                    run("P", ten.matmul(rep[:, e:NH:8], eye, T.F[:, lo + 7:hi:8], True, True))
+                return ten.matmul(rep[:, 7:NH:8], eye, T.F[:, lo + 7:hi:8], True, True)
+            if name == "sign":
+                return act.activation(T.S[:, c], rep[:, lo % NH:lo % NH + n], AF.Sign)
+            if name == "before":
+                return vec.tensor_tensor_scan(T.Pre[:, c], T.A[:, a - 1:a + n - 1], T.Z[:, 0:n], 0.0, OP.min, OP.max)
+            if name == "behind":
+                return vec.tensor_tensor_scan(T.Suf[:, hi - 1:lo - 1 if lo else None:-1], T.A[:, a + n:a:-1], T.Z[:, 0:n], 0.0, OP.min, OP.max)
+            if name == "first":
+                return act.activation(T.Pre[:, lo:hi:8], T.Suf[:, lo:hi:8], AF.Copy)
+            if name == "least":
+                return vec.tensor_tensor_scan(T.U[:, c], T.Suf[:, c], T.Pre[:, c], 0.0, OP.max, OP.min)
+            return vec.tensor_tensor_scan(T.Rc[:, c], T.S[:, c], T.U[:, c], 0.0, OP.add, OP.mult)
 
-        def fetch(q, lo, hi):
-            o, i = T.D[:, lo:hi], win.indirect(T.pl16[:, lo // 16:hi // 16])
-            edges[lo // NH].append(run("V", vec.tensor_copy(o, i)) if q == "V" else run("A", act.activation(o, i, AF.Copy)))
-
-        def sizes(k):
-            need("A", *edges[k])
-            ab[k] = run("A", act.activation(T.A[:, at[k]:at[k] + NH], part(T.D, k), AF.Abs, bias=-0.5 / K, scale=512 / K))
-
-        def product(k):
-            need("V", *edges[k])
-            f[k] = run("V", vec.tensor_tensor_scan(part(T.F, k), T.Zf[:, :], part(T.D, k), 0.0, OP.max, OP.mult))
-
-        def sign(k):
-            need("P", f[k])
-            for e in range(8):
-                t = run("P", ten.matmul(T["bk%d" % (2 + k)][:, e:NH:8], eye, T.F[:, k * NH + 7:(k + 1) * NH:8], True, True))
-            need("A", t)
-            sg[k] = run("A", act.activation(part(T.S, k), T["bk%d" % (2 + k)][:, :], AF.Sign))
-
-        def before(k):
-            need("V", ab[k])
-            pre[k] = run("V", vec.tensor_tensor_scan(part(T.Pre, k), T.A[:, at[k] - 1:at[k] + NH - 1], T.Z[:, :], 0.0, OP.min, OP.max))
-
-        def behind(k):
-            need("V", ab[k])
-            suf[k] = run("V", vec.tensor_tensor_scan(T.Suf[:, NJ - 1:NH - 1:-1] if k else T.Suf[:, NH - 1::-1], T.A[:, at[k] + NH:at[k]:-1],
-                                                     T.Z[:, :], 0.0, OP.min, OP.max))
-
-        def first(k):
-            need("V", pre[k], suf[k])
-            pre[k] = run("V", vec.tensor_copy(T.Pre[:, k * NH:(k + 1) * NH:8], T.Suf[:, k * NH:(k + 1) * NH:8]))
-
-        def both(lo, hi):
-            need("V", pre[lo // NH])
-            u[lo] = run("V", vec.tensor_tensor_scan(T.U[:, lo:hi], T.Suf[:, lo:hi], T.Pre[:, lo:hi], 0.0, OP.max, OP.min))
-
-        def signed(lo, hi):
-            need("V", u[lo], sg[lo // NH])
-            w[lo] = run("V", vec.tensor_tensor_scan(T.Rc[:, lo:hi], T.S[:, lo:hi], T.U[:, lo:hi], 0.0, OP.add, OP.mult))
-
-        fetch("V", NH, NH + G1)
-        fetch("A", NH + G1, NJ)
-        fetch("V", 0, G0)
-        sizes(1)
-        fetch("A", G0, NH)
-        sizes(0)
-        product(1)
-        sign(1)
-        for step, k in ((before, 1), (behind, 1), (product, 0), (sign, 0), (first, 1), (before, 0), (behind, 0)):
-            step(k)
-        for d in (RAW, 4):
+        todo = {q: list(CHECK[q]) for q in CHECK}
+        while any(todo.values()):
+            for q in todo:
+                while todo[q]:
+                    name, lo, hi = todo[q][0]
+                    if name == "list":
+                        if r == 0 and q == "P":
+                            need("P", late["E32"], ("dr", 32))
+                            run("P", ten.matmul(T.bk4[:, 0:80], T.E32[:, :], T.inva[:, :], True, False))
+                            inv[0] = run("P", ten.matmul(T.bk4[:, 0:80], T.E32[:, :], T.invb[:, :], False, True))
+                        elif r == 0:
+                            if not inv[0]:
+                                break
+                            need("V", inv[0])
+                            inv[0] = run("V", vec.tensor_scalar(T.inv16[:, :], T.bk4[:, 0:80], 0.25 - OFF, 0.0, OP.add, OP.max))
+                        todo[q].pop(0)
+                        continue
+                    src = [[m for m in made[n] if m[0] < hi and lo < m[1]] for n in READS[name]]
+                    if any(sum(min(hi, m[1]) - max(lo, m[0]) for m in ms) < hi - lo for ms in src):
+                        break
+                    todo[q].pop(0)
+                    need(q, *[m[2] for ms in src for m in ms])
+                    made[name].append((lo, hi, run(q, one(q, name, lo, hi))))
+        for d in (4, 1) if r else (RAW, 4, 1):
             own_sign(dwin, d, ev[d])
-        both(NH, NJ)
-        first(0)
-        signed(NH, NJ)
-        if r == 0:
-            need("V", ("dr", 32))
-            inv[0] = run("V", vec.tensor_tensor(T.inv32[:, :], T.inva[:, :], T.invb[:, :], OP.add))
-        both(0, NH // 2)
-        both(NH // 2, NH)
-        if r == 0:
-            need("V", inv[0])
-            inv[0] = run("V", vec.tensor_scalar(T.inv16[:, :], T.inv32[:, :], 0.25 - OFF, 0.0, OP.add, OP.max))
-        signed(0, NH // 2)
-        signed(NH // 2, NH)
+        sg = [bank(T["bk%d" % (5 + i)], 0) for i in range(2)]
+        for i in range(2 * r):
+            need("P", *late["got"])
+            run("P", ten.matmul(sg[i], T.NI[:, :], bank(T.Rv0, diff[i]), True, False))
+            t = run("P", ten.matmul(sg[i], eye, bank(T.Tg1, diff[i]), False, True))
         dst = T["Rs%d" % r]
-        got = by_slots(2 * r + 1, T.Rc[:, 0:NJ], T.inv16, (dst, T["Lr%d" % r], T["Xr%d" % r], T["Rv%d" % r]), [*w.values(), inv[0]])
+        got = by_slots(2 * r + 1, T.Rc[:, 0:NJ], T.inv16, (dst, T["Lr%d" % r], T["Xr%d" % r], T["Rv%d" % r]),
+                       [made["signed"][-1][2], inv[0]])
+        for i in range(2 * r):
+            need("A", t)
+            sv[0] = run("A", act.activation(bank(T.sv1, i), sg[i], AF.Sign, bias=0.5))
+        if r:
+            need("P", sv[0])
         if r == 0:
             for i in range(2):
                 so = run("A", act.activation(bank(T.so, i), bank(dwin, diff[i]), AF.Sign))
             for i in range(2):
                 sv[0] = run("A", act.activation(bank(T.sv0, i), bank(T.Tg0, diff[i]), AF.Sign, bias=0.5))
+            need("V", vl_in, ("rn", LIST[1]))
+            late["rn"] = run("V", vec.tensor_copy(T.rn16[:, :], T.rn32[:, :]))
+            late["vl"] = run("V", vec.tensor_copy(T.vl16[:, :], T.vl32[:, :]))
             need("V", so, *got.values())
             for i in range(2):
                 rf[0] = run("V", vec.tensor_tensor_scan(bank(T.Rf, i), bank(T.so, i), bank(dst, diff[i]), 0.0, OP.add, OP.mult))
@@ -376,47 +379,43 @@ def rank_program(g, core, T, topo):
         rv = T["Rv%d" % r]
         ev = taken(2 * r + 1, T["Rs%d" % r], rs, T["Lr%d" % r], rv)
         gd = T["Gv%d" % r]
-        need("V", vl16, *ev.values())
-        need("A", vl16, *ev.values())
+        need("V", late["vl"], *ev.values())
+        need("A", late["vl"], *ev.values())
 
         def piece(d, lo=0, hi=256):
             return gd[:, 256 * d + lo:256 * d + hi], rv[:, 0:W].indirect(T.vl16[:, 16 * d + lo // 16:16 * d + hi // 16])
 
-        o, i = piece(0)
-        g0 = run("V", vec.tensor_tensor(o, i, T.xs[:, :], OP.add))
-        g3 = [run("V", vec.tensor_copy(*piece(3, 128, 256)))]
-        g2 = run("A", act.activation(*piece(2), AF.Copy))
-        g3.append(run("A", act.activation(*piece(3, 0, 128), AF.Copy)))
-        need("V", g0)
-        o, i = piece(1)
-        g1 = run("V", vec.tensor_tensor(o, i, gd[:, 0:256], OP.add))
-        tt = T.bk0[:, 0:256]
-        need("P", ev[0], g2)
-        run("P", ten.matmul(tt, eye, gd[:, 512:768], True, False))
-        need("P", *g3)
-        t = run("P", ten.matmul(tt, eye, gd[:, 768:1024], False, True))
-        need("V", g1, t)
-        return run("V", vec.tensor_tensor(out[:, :], tt, gd[:, 256:512], OP.add))
+        a, b, held, ins = (0, VA), (VA, V), {}, {}
+
+        def add(d, lo, hi):
+            o, i = piece(d, lo, hi)
+            if d:
+                need("V", held[lo][1])
+            held[lo] = (o, run("V", vec.tensor_tensor(o, i, held[lo][0] if d else T.xs[:, lo:hi], OP.add)))
+
+        need("P", ev[0])
+        for d, (lo, hi), last in ((2, a, False), (3, a, True), (2, b, True)):
+            o, i = piece(d, lo, hi)
+            need("P", run("A", act.activation(o, i, AF.Copy)))
+            ins[lo] = run("P", ten.matmul(T["bk%d" % (lo > 0)][:, 0:hi - lo], eye, o, d == 2, last))
+        for d, part in ((0, b), (0, a), (1, b), (1, a), (3, b)):
+            add(d, *part)
+        for lo, hi in (a, b):
+            need("V", held[lo][1], ins[lo])
+            t = run("V", vec.tensor_tensor(out[:, lo:hi], T["bk%d" % (lo > 0)][:, 0:hi - lo], held[lo][0], OP.add))
+        return t
 
     rs = check(0, own)
     tw = variables(0, rs, T.Tw)
     need("G", tw)
     send_raw(2, T.Tw)
-    need("P", ni, tw)
-    sg = [bank(T["bk%d" % (6 + i)], 0) for i in range(2)]
-    for i in range(2):
-        run("P", ten.matmul(sg[i], T.NI[:, :], bank(T.Rv0, diff[i]), True, False))
-    less_own((2, 3, RAW))
+    need("P", tw)
+    less_own((RAW, 7, 3, 2, 6))
     got = by_slots(2, T.Tw[:, 0:256], T.sn16, (T.Tg1, T.Lm1, T.Xm1, T.Dw1), [tw])
-    need("P", *got.values())
-    for i in range(2):
-        t = run("P", ten.matmul(sg[i], eye, bank(T.Tg1, diff[i]), False, True))
-        need("A", t)
-        sv[0] = run("A", act.activation(bank(T.sv1, i), sg[i], AF.Sign, bias=0.5))
+    late["got"] = list(got.values())
     gather_raw(2)
     rs = check(1, got[0])
-    yt = variables(1, rs, T.ys)
-    need("S", yt)
+    need("S", variables(1, rs, T.ys))
     g.sync.dma_start(T.y[:, :], T.ys[:, :]).then_inc(T.sem.dy, 16)
     need("S", ("dy", 16))
     for q in ("V", "A", "P", "G"):

@@ -3,72 +3,120 @@ from concourse.mybir import dt, AluOpType, AxisListType, ActivationFunctionType
 
 NR, CAP, V, M = 8, 160, 256, 128
 W = NR * CAP
-BK = 2 * CAP
-H = 2 * BK
+H = 4 * CAP
 NJ = 8 * M
 NH = NJ // 2
-PC = 256
-VA = 192
+VA = 160
 B = 51.0
 K = float(2 ** 20)
+BIG = float(2 ** 90)
 OFF = 64
 OP = AluOpType
 AF = ActivationFunctionType
+FREE = (2, 6)
+AT_V = [4 * (p ^ 6) % 8 if p >= 4 else 0 for p in range(NR)]
+AT_C = [(AT_V[q ^ 2] - q * (q ^ 2)) % 8 for q in range(NR)]
 RAW = 5
-TO_CHECKS = {"V": "g7 g4 g1 g0 c1", "A": "g3 g2 g6 c4", "recv": "V0 s0 A5 s5 V7 A3 A2 V6",
-             "calls": [[(5, 0, 8)], [(7, 0, 4), (3, 4, 4)], [(6, 0, 4), (2, 4, 4)], [(4, 0, 4), (1, 4, 4)]]}
-PART = {"a": (0, 64), "b": (64, CAP)}
-TO_VARS = {"V": "a3 g5 g4 g1 g0 c1", "A": "b3 g7 g2 g6 c4", "recv": "A0 V3 V7 A5 V2 V6",
-           "calls": [[(3, 0, 8)], [(7, 0, 4), (5, 4, 4)], [(2, 0, 4), (6, 4, 4)], [(4, 0, 4), (1, 4, 4)]]}
-LIST = (0, 8)
-FIRST = dict(TO_CHECKS, V="a5 g7 x0 g4 x1 g1 x2 c4 x3 c1", A="b5 g3 g2 g6 g0 n0", recv="A5 V0 V7 A3 V2 A6")
-SV = 512
-PLAN = {0: FIRST, 1: dict(TO_VARS, A="b3 g7 g2 s0 g6 c4"), 2: TO_CHECKS, 3: TO_VARS}
-READS = {"edges": [], "size": ["edges"], "product": ["edges"], "repeat": ["product"], "sign": ["repeat"], "before": ["size"],
-         "behind": ["size"], "first": ["before", "behind"], "least": ["first"], "signed": ["least", "sign"]}
-
-
-H0, H1 = (0, NH), (NH, NJ)
-Q0, Q1, Q2, Q3 = [(a, a + PC) for a in range(0, NJ, PC)]
-CHECK = {"V": [("edges", *Q0), ("edges", 512, 640), ("product", *H0), ("edges", 640, 768), ("before", *Q0), ("behind", *Q0), ("product", *H1)]
-         + [(n, *q) for q in (Q1, Q2, Q3) for n in ("before", "behind")]
-         + [("least", *H0), ("least", *Q2), ("least", *Q3), ("list", 0, 0), ("signed", *H0), ("signed", *H1)],
-         "A": [("edges", *Q1), ("edges", 768, 864), ("size", *Q0), ("edges", 864, NJ), ("size", *Q1), ("size", *Q2), ("size", *Q3),
-               ("sign", *Q0), ("first", *H0), ("sign", *Q1), ("first", *Q2), ("first", *Q3), ("sign", *H1)],
-         "P": [("repeat", *H0), ("repeat", *H1), ("list", 0, 0)]}
+OFFCHIP = 8
+PART = {"g": (0, 10)}
+FIRST = {"V": "x0 g2 x1 g7 x2 g4 x3 g0 c1", "A": "g3 g5 g1 n6 g6", "recv": "V0 A3 V7 A5 V4",
+         "calls": [[(3, 0, 8), (2, 8, 8)], [(7, 0, 8)], [(5, 0, 8)], [(4, 0, 8)], [(1, 0, 4), (6, 4, 4)]]}
+SECOND = {"V": "g2 g7 g1 g6 g0", "A": "g3 g4 c1 g5", "recv": "A0 s0 A5 A3 V7 A4",
+          "calls": [[(5, 0, 8)], [(3, 0, 8), (2, 8, 8)], [(7, 0, 8)], [(4, 0, 8)], [(6, 0, 8)], [(1, 0, 8)]]}
+TO_VARS = {"V": "g2 g4 g1 g0 g6", "A": "s2 s4 k2 s6 g3 g7 g5 k6 c4", "recv": "A0 V3 V7 V5 V1",
+           "calls": [[(3, 0, 8), (2, 8, 8)], [(7, 0, 8)], [(5, 0, 8)], [(1, 0, 8)], [(4, 0, 4), (6, 4, 4)]]}
+PLAN = {0: FIRST, 1: dict(TO_VARS, V="g2 g4 g1 g6 g0", A="s2 s4 s6 g3 g7 g5 c4 s0"), 2: SECOND, 3: TO_VARS}
+ON = {"rn": (0, 8), 0: (0, 8), 1: (0, 8), 2: (0, 8), 3: (0, 8)}
+LIST = (8, 8)
+SV = 480
+LESS = (3, 5)
+READS = {"edges": [], "size": ["edges"], "product": ["edges"], "repeat": ["product"], "sign": ["repeat"],
+         "before": ["size"], "behind": ["size"], "first": ["before", "behind"], "least": ["first"], "signed": ["least", "sign"],
+         "sum": [], "list": ["sum"]}
+H0, H1, ALL = (0, NH), (NH, NJ), (0, NJ)
+Q0, Q1, Q2, Q3 = (0, 256), (256, NH), (NH, 864), (864, NJ)
+CHECK = {"V": [("edges", 0, 288), ("edges", 512, 640), ("product", *H0), ("edges", 640, 768), ("behind", *Q0), ("before", *Q0), ("product", *H1)]
+         + [(n, *q) for q in (Q1, Q2) for n in ("behind", "before")] + [("before", *Q3), ("behind", *Q3)]
+         + [("least", *H0), ("first", *Q3), ("least", *Q2), ("least", *Q3), ("signed", *H0), ("list", *ALL), ("signed", *H1)],
+         "A": [("edges", 288, 512), ("edges", 768, 928), ("size", *Q0), ("edges", 928, NJ), ("size", *Q1), ("size", *Q2), ("size", *Q3),
+               ("sign", *Q0), ("first", *H0), ("sign", *Q1), ("first", *Q2), ("sign", *H1)],
+         "P": [("repeat", *H0), ("repeat", *H1), ("sum", *ALL)]}
 
 SCRATCH = {
     "sn32": ("sbuf", [128, 80], "int32"), "pl32": ("sbuf", [128, 64], "int32"), "vl32": ("sbuf", [128, 64], "int32"),
     "sn16": ("sbuf", [128, 80], "uint16"), "pl16": ("sbuf", [128, 64], "uint16"), "vl16": ("sbuf", [128, 64], "uint16"),
-    "pm32": ("sbuf", [128, 64], "int32"), "ln32": ("sbuf", [128, 10], "int32"), "rn32": ("sbuf", [128, 10], "int32"), "rn16": ("sbuf", [128, 10], "uint16"),
+    "pm32": ("sbuf", [128, 64], "int32"), "ln32": ("sbuf", [128, 10], "int32"), "rn32": ("sbuf", [128, 10], "int32"),
+    "rn16": ("sbuf", [128, 10], "uint16"), "hl": ("sbuf", [128, 10], "int32"), "hx": ("sbuf", [128, 4 * CAP], "bfloat16"),
+    "hd": ("dram", [4 * 256, CAP], "bfloat16"),
     "ta": ("sbuf", [128, 64], "int32"), "tb": ("sbuf", [128, 64], "int32"), "tc": ("sbuf", [128, 64], "int32"),
     "td": ("sbuf", [128, 64], "int32"), "pc16": ("sbuf", [128, 64], "uint16"),
     "num": ("sbuf", [128, NJ], "float32"),
     "iva": ("sbuf", [128, W], "float32"), "ivb": ("sbuf", [128, W], "float32"),
     "inva": ("sbuf", [128, 80], "float32"), "invb": ("sbuf", [128, 80], "float32"), "nil": ("sbuf", [128, 320], "float32"),
     "inv16": ("sbuf", [128, 80], "uint16"),
-    "one": ("sbuf", [128, 128], "bfloat16"), "E": ("sbuf", [128, 256], "bfloat16"), "NI": ("sbuf", [128, 128], "bfloat16"),
-    "EK": ("sbuf", [128, 256], "bfloat16"), "NK": ("sbuf", [128, 128], "bfloat16"),
-    "xs": ("sbuf", [128, 256], "bfloat16"), "Tw": ("sbuf", [128, 256], "bfloat16"), "E32": ("sbuf", [128, 128], "float32"), "ys": ("sbuf", [128, 256], "float32"),
-    "D": ("sbuf", [128, NJ], "bfloat16"), "A": ("sbuf", [128, NJ + NJ // PC + 1], "bfloat16"), "F": ("sbuf", [128, NJ], "bfloat16"),
+    "E": ("sbuf", [128, 256], "bfloat16"), "NI": ("sbuf", [128, 128], "bfloat16"),
+    "EK": ("sbuf", [128, 256], "bfloat16"), "E32": ("sbuf", [128, 128], "float32"),
+    "xs": ("sbuf", [128, V], "bfloat16"), "xk": ("sbuf", [128, V], "bfloat16"), "Tw": ("sbuf", [128, V], "bfloat16"),
+    "rx": ("sbuf", [128, V], "bfloat16"), "ys": ("sbuf", [128, V], "float32"),
     "Z": ("sbuf", [128, NH], "bfloat16"), "Zf": ("sbuf", [128, NH], "bfloat16"),
-    "Pre": ("sbuf", [128, NJ], "bfloat16"), "Suf": ("sbuf", [128, NJ], "bfloat16"),
-    "S": ("sbuf", [128, NJ], "bfloat16"), "U": ("sbuf", [128, NJ], "bfloat16"), "Rc": ("sbuf", [128, NJ], "bfloat16"),
-    "sc": ("sbuf", [128, H], "bfloat16"), "so": ("sbuf", [128, H], "bfloat16"), "Rf": ("sbuf", [128, H], "bfloat16"),
 }
+for _n in ("D", "A", "F", "Pre", "Suf", "S", "U", "Rc"):
+    SCRATCH[_n] = ("sbuf", [128, NJ], "bfloat16")
+for _n in ("sc", "sk", "so", "Rf"):
+    SCRATCH[_n] = ("sbuf", [128, H], "bfloat16")
 for _d in range(NR):
     SCRATCH["bk%d" % _d] = ("psum", [128, 512], "float32")
 for _r in range(2):
-    for _n, _w in (("Tg", W), ("Rs", W), ("Lm", W), ("Lr", W), ("Xm", W), ("Xr", W), ("Dw", W), ("Rv", W), ("Gv", 1024), ("sv", H),
-                   ("rx", 256)):
+    for _n, _w in (("Tg", W), ("Rs", W), ("Lm", W), ("Lr", W), ("Xm", W), ("Xr", W), ("Dw", W), ("Rv", W), ("Gv", 1024), ("sv", H)):
         SCRATCH["%s%d" % (_n, _r)] = ("sbuf", [128, _w], "bfloat16")
-SEMAPHORES = ["sV", "sA", "sP", "sG", "dl", "dx", "dpm", "dsn", "dpl", "dvl", "df", "dr", "dy", "ls", "rn"]
-SEMAPHORES += ["arr%d_%d" % (ph, p) for ph in range(4) for p in range(NR)]
+SEMAPHORES = ["sV", "sA", "sP", "sG", "dl", "dx", "dpm", "dsn", "dpl", "dvl", "df", "dr", "dy", "ls", "rn", "hl"]
+SEMAPHORES += ["arr%d_%d" % (ph, p) for ph in range(4) for p in range(NR)] + ["hop%d" % ph for ph in range(4)]
+
+
+def blk(buf, q):
+    return buf[:, q * CAP:(q + 1) * CAP]
+
+
+def helper(topo, cores, c):
+    return [h for h in topo.cores_of(c) if topo.die(h) != topo.die(c) and all(topo.may_write(h, o) for o in cores)][0]
+
+
+def shift(ph, src, dst):
+    p, q = (dst, src) if ph % 2 else (src, dst)
+    return (p * q + AT_C[q] - AT_V[p]) * (-1 if ph % 2 else 1) % 8
+
+
+def handed(ph):
+    return [d for call in PLAN[ph]["calls"] for d, o, n in call if o >= OFFCHIP][0]
+
+
+def hop(T, ph, r):
+    k = shift(ph, r, r ^ handed(ph))
+    if not k:
+        return [blk(T.hx, ph)], blk(T.hx, ph)
+    o = 256 * ph
+    return [T.hd[o:o + 128, :], T.hd[o + 128:o + 256, :]], T.hd[o + 128 - 16 * k:o + 256 - 16 * k, :]
+
+
+def hand_on(g, core, T, topo, r):
+    jobs = [(RAW, T.hl[:, :], "hl", LIST[1], T.rn32[:, :], "rn", ON["rn"])]
+    for ph in range(4):
+        there, on = hop(T, ph, r)
+        jobs.append((handed(ph), on, "hop%d" % ph, 8 * len(there), blk(T[("Dw%d", "Rv%d")[ph % 2] % (ph // 2)], r), "arr%d_%d" % (ph, r), ON[ph]))
+    for d, src, sem, n, dst, arr, (o, k) in jobs:
+        to = T.cores[r ^ d]
+        rid, pid, _s = topo.addr(to)
+        g.wait_ge(T.sem[sem], n)
+        g.remote_dma(dst, src, T.sem[arr], T.sem.ls, pid, rid, sum(1 << e for e in topo.engines(core, to)[o:o + k]))
+    g.wait_ge(T.sem.ls, sum(j[-1][1] for j in jobs))
 
 
 def rank_program(g, core, T, topo):
     me = T.rank_of(core)
     if me is None:
+        for r, c in enumerate(T.cores):
+            if helper(topo, T.cores, c) == core:
+                hand_on(g, core, T, topo, r)
         return
     queue = {"V": g.vector, "A": g.scalar, "P": g.tensor, "G": g, "S": g.sync}
     cnt = {"V": 0, "A": 0, "P": 0, "G": 0, "ls": 0}
@@ -86,27 +134,20 @@ def rank_program(g, core, T, topo):
         inst.then_inc(T.sem["s" + q], 1)
         return ("s" + q, cnt[q])
 
-    s0 = me // 2
-    same = [s0, s0 ^ 2]
-    diff = [s0 ^ 1, s0 ^ 3]
-
-    def bank(buf, b):
-        return buf[:, b * BK:(b + 1) * BK]
-
-    def blk(buf, q):
-        return buf[:, q * CAP:(q + 1) * CAP]
-
-    def half(buf, q):
-        b = q // 2
-        return blk(buf, 2 * (same.index(b) if b in same else diff.index(b)) + q % 2)
-
     def ps(d):
         return T["bk%d" % d][:, 0:CAP]
 
-    def turn(ph, r):
-        k = me * r if ph % 2 == 0 else -me * r
-        s = (128 - 16 * (k % 8)) % 128
-        return (T.EK if ph % 2 else T.E)[:, s:s + 128]
+    def turn(ph, r, sender):
+        s = (128 - 16 * (shift(ph, me, r) if sender else shift(ph, r, me))) % 128
+        return (T.EK if ph == 3 else T.E)[:, s:s + 128]
+
+    def move(sb, hbm, k, sem, store=False, queues="SS", rows=lambda a, b: slice(a, b)):
+        for q, (a, b, o) in zip(queues, ((0, 128 - 16 * k, 16 * k), (128 - 16 * k, 128, 16 * k - 128))):
+            if a < b:
+                sides = sb[0][a + o:b + o, sb[1]], hbm[0][rows(a, b), hbm[1]]
+                queue[q].dma_start(*sides[::-1] if store else sides).then_inc(T.sem[sem], 16)
+                cnt[sem] = cnt.get(sem, 0) + 16
+        return (sem, cnt[sem])
 
     def places(i):
         need("V", pc[0] or pl_in)
@@ -120,32 +161,28 @@ def rank_program(g, core, T, topo):
         else:
             pc[0] = run("V", vec.tensor_copy(T.pc16[:, :], T.td[:, :]))
 
-    eye, pc = T.E[:, 0:128], [None]
-    act.dma_start(T.ln32[:, :], T.sn[:, (me ^ RAW) * 10:(me ^ RAW) * 10 + 10]).then_inc(T.sem.dl, 16)
-    g.sync.dma_start(T.sn32[:, :], T.sn[:, :]).then_inc(T.sem.dsn, 16)
-    g.sync.dma_start(T.xs[:, 0:256], T.x[:, :]).then_inc(T.sem.dx, 16)
-    g.sync.dma_start(T.pl32[:, :], T.pl[:, :]).then_inc(T.sem.dpl, 16)
-    sn_in, x_in, pl_in, pm_in, vl_in = ("dsn", 16), ("dx", 16), ("dpl", 16), ("dpm", 128), ("dvl", 16)
+    eye, pc, whole, kv, kc = T.E[:, 0:128], [None], slice(None), AT_V[me], AT_C[me]
+    ln_in = move((T.ln32, whole), (T.sn, slice((me ^ RAW) * 10, (me ^ RAW) * 10 + 10)), kv, "dl", queues="AA")
+    sn_in = move((T.sn32, whole), (T.sn, whole), kv, "dsn")
+    pl_in = move((T.pl32, whole), (T.pl, whole), kc, "dpl", queues="AA")
+    x_in = move((T.xs, whole), (T.x, whole), kv, "dx")
     num = run("G", g.iota(T.num[:, 0:256], [[1, 2], [8, 16], [128, 8]], OFF, 0, allow_small_or_imprecise_dtypes=True))
-    ones = run("V", vec.memset(T.one[:, :], 1.0))
-    need("G", ones)
-    eye1 = run("G", g.affine_select(eye, T.one[:, :], [[-1, 128]], OP.is_equal, 0.0, 0, 1))
-    need("A", ones)
-    run("A", act.activation(T.A[:, 0::PC + 1], T.one[:, 0:NJ // PC + 1], AF.Silu))
+    z = [run("V", vec.memset(T.Zf[:, :], -BIG))]
+    need("A", *z)
+    z = [run("A", act.activation(T.Zf[:, 0:NH:8], T.Zf[:, 0:NH:8], AF.Silu, scale=-1.0))]
     fill = run("V", vec.memset(T.nil[:, :], 0.0))
-    need("S", fill)
-    for win in (T.iva, T.ivb):
-        g.sync.dma_start(win[0:128:16, :], T.nil[0:32, :]).then_inc(T.sem.df, 16)
+    need("G", fill)
+    eyes = run("G", g.affine_select(T.E[:, :], T.nil[:, 0:256], [[0, 2], [-1, 128]], OP.not_equal, 1.0, 0, 1))
     for u in range(8):
-        g.sync.dma_start(T.pm32[:, 8 * u:8 * u + 8], T.pl[u:128:8, :]).then_inc(T.sem.dpm, 16)
-    z = [run("V", vec.memset(T.Zf[:, :], -1.0)), run("V", vec.memset(T.Z[:, :], 0.0))]
+        if u == 3:
+            need("S", fill)
+            for win in (T.iva, T.ivb):
+                g.sync.dma_start(win[0:128:16, :], T.nil[0:32, :]).then_inc(T.sem.df, 16)
+        pm_in = move((T.pm32, slice(8 * u, 8 * u + 8)), (T.pl, whole), kc, "dpm", rows=lambda a, b: slice(a + u, b, 8))
+    z.append(run("V", vec.memset(T.Suf[:, 7:NJ:8], B / K)))
     need("V", num)
-    num = run("V", vec.tensor_scalar(T.num[:, 256:512], T.num[:, 0:256], 2.0, None, OP.add))
-    need("V", *z)
-    z = [run("V", vec.memset(T.Zf[:, 0:NH:8], 1.0)), run("V", vec.memset(T.Z[:, 0:NH:8], B / K))]
-    need("V", eye1)
-    eyes = run("V", vec.tensor_copy(T.E[:, 128:256], eye))
-    num2 = run("V", vec.tensor_scalar(T.num[:, 512:768], T.num[:, 0:256], 4.0, None, OP.add))
+    for e in (2, 4):
+        num = run("V", vec.tensor_scalar(T.num[:, 128 * e:128 * e + 256], T.num[:, 0:256], float(e), None, OP.add))
     need("V", sn_in)
     sn16 = run("V", vec.tensor_copy(T.sn16[:, :], T.sn32[:, :]))
 
@@ -156,136 +193,123 @@ def rank_program(g, core, T, topo):
         return [d for q in "VA" for k, d in toks(ph, q, "c")]
 
     def arrived(ph, d):
-        return ("arr%d_%d" % (ph, me ^ d), [n for c in PLAN[ph]["calls"] for e, o, n in c if e == d][0])
+        return ("arr%d_%d" % (ph, me ^ d), [n if o < OFFCHIP else ON[ph][1] for c in PLAN[ph]["calls"] for e, o, n in c if e == d][0])
 
     def send(items):
         tr = []
         for d, o, n, src, dst, sem in items:
-            to = T.cores[me ^ d]
+            to = T.cores[me ^ d] if o + n <= OFFCHIP else helper(topo, T.cores, core)
             rid, pid, _s = topo.addr(to)
-            tr.append(RemoteDMATransfer(dst_ids=[DstId(rid=rid, pnc=pid)], dma_engine_mask=sum(1 << e for e in topo.engines(core, to)[o:o + n]),
-                                        remote_sem=T.sem[sem], src=src, dst=dst))
+            tr.append(RemoteDMATransfer(dst_ids=[DstId(rid=rid, pnc=pid)] * len(dst), remote_sem=T.sem[sem], src=src, dsts=dst,
+                                        dma_engine_mask=sum(1 << e for e in topo.engines(core, to)[o:o + n])))
             cnt["ls"] += n
         g.remote_dma_fused(tr, local_sem=T.sem.ls)
 
-    def send_raw(ph, win):
-        d, o, n = PLAN[ph]["calls"][0][0]
-        send([(d, o, n, win[:, :], T["rx%d" % (ph // 2)][:, :], "arr%d_%d" % (ph, me))])
-
-    def drain(ph, q, out, src):
-        if ph % 2 == 0:
-            if q == "V":
-                return run("V", vec.tensor_scalar(out, src, 1.0 / 512, 1.0 / 1024, OP.mult, OP.add))
-            return run("A", act.activation(out, src, AF.Identity, bias=1.0 / 1024, scale=1.0 / 512))
-        if q == "V":
-            return run("V", vec.tensor_copy(out, src))
-        return run("A", act.activation(out, src, AF.Copy))
+    def drain(q, out, src):
+        return run("V", vec.tensor_copy(out, src)) if q == "V" else run("A", act.activation(out, src, AF.Copy))
 
     def by_slots(ph, win, lst, bufs, ready):
         src, land, xsrc, xland = bufs
         xs, got, out, trn = turned_here(ph), {}, {}, {}
-        need("V", *ready)
-        need("A", *ready)
 
         def gather(q, d, lo, hi):
             r = me ^ d
-            i, o = win.indirect(lst[:, (r * CAP + lo) // 16:(r * CAP + hi) // 16]), src[:, r * CAP + lo:r * CAP + hi]
+            need(q, *ready)
+            i, o = win.indirect(lst[:, r * 10 + lo:r * 10 + hi]), src[:, r * CAP + 16 * lo:r * CAP + 16 * hi]
+            if ph == 0:
+                if q == "A":
+                    return run("A", act.activation(o, i, AF.Identity, bias=0.5 / K, scale=1 / K))
+                return run("V", vec.tensor_scalar(o, i, 0.5, 1 / K, OP.add, OP.mult))
             if q == "A":
                 return run("A", act.activation(o, i, AF.Copy))
-            if ph == 2 and not d & 2:
+            if ph == 2:
                 return run("V", vec.tensor_tensor(o, i, blk(T.Rv0, r), OP.subtract))
-            if ph % 2 and not d & 2:
+            if d % 2 == 0:
                 need("V", sc[d])
-                return run("V", vec.tensor_tensor(o, i, half(T.sc, r), OP.mult))
+                return run("V", vec.tensor_tensor(o, i, blk(T.sk if ph == 3 and d in (*FREE, handed(ph)) else T.sc, d // 2), OP.mult))
             return run("V", vec.tensor_copy(o, i))
 
         todo = {q: toks(ph, q) for q in "VA"}
         while todo["V"] or todo["A"]:
             for q in "VA":
-                while todo[q] and (todo[q][0][1] in trn if todo[q][0][0] == "c" else
-                                   q == "A" or ph % 2 == 0 or todo[q][0][1] & 2 or todo[q][0][1] in sc):
-                    kind, d = todo[q].pop(0)
+                while todo[q]:
+                    kind, d = todo[q][0]
+                    if d not in trn if kind == "c" else q == "V" and ph % 2 and d % 2 == 0 and (d not in sc or ("k", d) in todo["A"]):
+                        break
+                    todo[q].pop(0)
                     r = me ^ d
                     if kind == "n":
                         need("A", num)
-                        late["num"] = run("A", act.activation(T.num[:, 768:NJ], T.num[:, 256:512], AF.Identity, bias=4.0))
-                        continue
-                    if kind == "x":
+                        late["num"] = run("A", act.activation(T.num[:, 128 * d:NJ], T.num[:, 0:256], AF.Identity, bias=float(d)))
+                    elif kind == "x":
                         places(d)
-                        continue
-                    if kind == "s":
+                    elif kind == "s":
                         own_sign(T["Dw%d" % (ph // 2)], d, late["ev"][d])
-                        continue
-                    if kind == "c":
+                    elif kind == "k":
+                        times_k(d)
+                    elif kind == "c":
                         need(q, trn[d])
-                        out[d] = drain(ph, q, blk(xsrc, r), ps(d))
-                        continue
-                    if kind != "g":
-                        out.setdefault("first", []).append(gather(q, d, *PART[kind]))
-                    got[d] = gather(q, d, 0, CAP) if kind == "g" else out["first"][-1]
-                    if d in xs:
-                        need("P", late["EK"] if ph % 2 else eyes, got[d])
-                        trn[d] = run("P", ten.matmul(ps(d), turn(ph, r), blk(src, r), True, True))
+                        out[d] = drain(q, blk(xsrc, r), ps(d))
+                    else:
+                        got[d] = out[d, kind] = gather(q, d, *PART[kind])
+                        if d in xs:
+                            need("P", late["EK"] if ph == 3 else eyes, got[d])
+                            trn[d] = run("P", ten.matmul(ps(d), turn(ph, r, True), blk(src, r), True, True))
         for c in PLAN[ph]["calls"][int(ph == 2):]:
-            for d, o, n in c:
-                need("G", out[d] if d in xs else got[d], *out.get("first", []))
-            send([(d, o, n, blk(xsrc if d in xs else src, me ^ d), blk(xland if d in xs else land, me), "arr%d_%d" % (ph, me))
+            need("G", *[out[k] for d, o, n in c for k in ([d] if d in xs else [(d, part) for part in PART]) if k in out])
+            send([(d, o, n, blk(xsrc if d in xs else src, me ^ d),
+                   *((hop(T, ph, me)[0], "hop%d" % ph) if o >= OFFCHIP else ([blk(xland if d in xs or d in FREE else land, me)], "arr%d_%d" % (ph, me))))
                   for d, o, n in c])
         return got
 
     def own_sign(dwin, d, there):
         need("A", there)
-        sc[d] = run("A", act.activation(half(T.sc, me ^ d), blk(dwin, me ^ d), AF.Sign))
+        sc[d] = run("A", act.activation(blk(T.sc, d // 2), blk(dwin, me ^ d), AF.Sign))
+
+    def times_k(d):
+        need("A", sc[d])
+        sc[d] = run("A", act.activation(blk(T.sk, d // 2), blk(T.sc, d // 2), AF.Identity, scale=K))
 
     def taken(ph, mine, mine_ready, land, rv):
         done, ev = {}, {}
         for q, d in [t for t in toks(ph, "recv") if t[0] != "s"]:
             p = me ^ d
-            need("P", rawg[ph] if (ph, d) == (2, RAW) else arrived(ph, d) if d else mine_ready)
-            done[d] = run("P", ten.matmul(ps(d), turn(ph, p), blk(land if d else mine, p), not (ph == 2 and (d & 2 or d == RAW)), True))
+            need("P", late["EK"] if ph == 3 else eyes, late["raw"] if (ph, d) == (2, RAW) else arrived(ph, d) if d else mine_ready)
+            done[d] = run("P", ten.matmul(ps(d), turn(ph, p, False), blk(land if d else mine, p), not (ph == 2 and d in (4, *LESS)), True))
         for q, d in toks(ph, "recv"):
             p = me ^ d
             if q == "s":
                 own_sign(rv, d, ev[d])
                 continue
             need(q, done[d])
-            if ph % 2 and d & 2:
-                need("V", sv[0])
-                ev[d] = run("V", vec.tensor_tensor(blk(rv, p), ps(d), half(T["sv%d" % (ph // 2)], p), OP.mult))
+            if ph % 2 and d % 2:
+                need("V", sv[d])
+                ev[d] = run("V", vec.tensor_tensor(blk(rv, p), ps(d), blk(T["sv%d" % (ph // 2)], d // 2), OP.mult))
             else:
-                ev[d] = drain(ph, q, blk(rv, p), ps(d))
-        for d in turned_here(ph):
+                ev[d] = drain(q, blk(rv, p), ps(d))
+        for d in (*turned_here(ph), *FREE, handed(ph)):
             ev[d] = arrived(ph, d)
         return ev
 
-    def gather_raw(ph):
-        need("V", late["rn"], arrived(ph, RAW))
-        win = T["rx%d" % (ph // 2)][:, 0:256]
-        rawg[ph] = run("V", vec.tensor_copy(blk(T["Lm%d" % (ph // 2)], me ^ RAW), win.indirect(T.rn16[:, :])))
-
-    inv, rf, sv, rawg, sc, late = [None], [None], [None], {}, {}, {}
-    need("G", ("dl", 16))
-    send([(RAW, *LIST, T.ln32[:, :], T.rn32[:, :], "rn")])
-    own = by_slots(0, T.xs[:, 0:256], T.sn16, (T.Tg0, T.Lm0, T.Xm0, T.Dw0), [sn16, x_in])[0]
-    need("V", pc[0], num2, ("df", 32))
+    inv, rf, sv, sc, late = [None], {}, {}, {}, {}
+    need("G", ln_in)
+    send([(RAW, *LIST, T.ln32[:, :], [T.hl[:, :]], "hl")])
+    own = by_slots(0, T.xs[:, :], T.sn16, (T.Tg0, T.Lm0, T.Xm0, T.Dw0), [sn16, x_in])[0]
+    need("V", pc[0], num, ("df", 32))
     scat = run("V", vec.tensor_copy(T.iva[:, 0:W].indirect(T.pc16[:, 0:SV // 16]), T.num[:, 0:SV]))
-    need("G", fill)
-    for o, n, s in ((T.E32, 1, 1.0), (T.EK, 2, K), (T.NI, 1, -1.0), (T.NK, 1, -K)):
+    for a in (0, 256):
+        z.append(run("G", g.affine_select(T.Z[:, a:a + 256], T.nil[:, 0:256], [[0, 32], [1, 8]], OP.not_equal, B / K, 0, 0)))
+    for o, n, s in ((T.E32, 1, 1.0), (T.NI, 1, -1.0), (T.EK, 2, K)):
         late[o.name] = run("G", g.affine_select(o[:, :], T.nil[:, 0:128 * n], [[0, n], [-1, 128]], OP.not_equal, s, 0, 1))
-    need("A", pc[0], num2, late["num"], ("df", 32))
+    need("A", pc[0], late["num"], ("df", 32))
     scat2 = run("A", act.activation(T.ivb[:, 0:W].indirect(T.pc16[:, SV // 16:64]), T.num[:, SV:NJ], AF.Silu))
     need("S", scat)
     g.sync.dma_start(T.inva[:, :], T.iva[0:128:16, :]).then_inc(T.sem.dr, 16)
     need("S", scat2)
     g.sync.dma_start(T.invb[:, :], T.ivb[0:128:16, :]).then_inc(T.sem.dr, 16)
-    g.sync.dma_start(T.vl32[:, :], T.vl[:, :]).then_inc(T.sem.dvl, 16)
+    vl_in = move((T.vl32, whole), (T.vl, whole), kv, "dvl")
     need("V", pm_in)
     pl16 = run("V", vec.tensor_copy(T.pl16[:, :], T.pm32[:, :]))
-
-    def less_own(ds):
-        need("P", late["NK"], rf[0])
-        for d in ds:
-            run("P", ten.matmul(ps(d), T.NK[:, :], half(T.Rf, me ^ d) if d & 2 else blk(T.Rs0, me ^ d), True, False))
 
     def check(r, mine_ready):
         dwin = T["Dw%d" % r]
@@ -295,19 +319,23 @@ def rank_program(g, core, T, topo):
         need("V", pl16, *ev.values())
         need("A", pl16, *ev.values())
         need("V", *z)
-
+        sg = {d: (blk(T["Tg%d" % r], me ^ d), []) for d in (3, 7, 5, 1)}
+        for i, d in enumerate(LESS * r):
+            need("P", *late["got"])
+            run("P", ten.matmul(ps(FREE[i]), T.NI[:, :], blk(T.Rv0, me ^ d), True, False))
+            sg[d] = ps(FREE[i]), [run("P", ten.matmul(ps(FREE[i]), eye, blk(T.Tg1, me ^ d), False, True))]
         made = {n: [] for n in READS}
 
         def one(q, name, lo, hi):
-            c, n, a = slice(lo, hi), hi - lo, 1 + lo + lo // PC
-            rep = T["bk%d" % (2 + lo // NH)]
+            c, n = slice(lo, hi), hi - lo
             if name == "edges":
                 o, i = T.D[:, c], win.indirect(T.pl16[:, lo // 16:hi // 16])
                 return vec.tensor_copy(o, i) if q == "V" else act.activation(o, i, AF.Copy)
             if name == "size":
-                return act.activation(T.A[:, a:a + n], T.D[:, c], AF.Abs, bias=-0.5 / K, scale=512 / K)
+                return act.activation(T.A[:, c], T.D[:, c], AF.Abs, bias=-0.5 / K)
             if name == "product":
                 return vec.tensor_tensor_scan(T.F[:, c], T.Zf[:, 0:n], T.D[:, c], 0.0, OP.max, OP.mult)
+            rep = T["bk%d" % (3 + lo // NH)]
             if name == "repeat":
                 for e in range(7):
                     run("P", ten.matmul(rep[:, e:NH:8], eye, T.F[:, lo + 7:hi:8], True, True))
@@ -315,109 +343,98 @@ def rank_program(g, core, T, topo):
             if name == "sign":
                 return act.activation(T.S[:, c], rep[:, lo % NH:lo % NH + n], AF.Sign)
             if name == "before":
-                return vec.tensor_tensor_scan(T.Pre[:, c], T.A[:, a - 1:a + n - 1], T.Z[:, 0:n], 0.0, OP.min, OP.max)
+                return vec.tensor_tensor_scan(T.Pre[:, lo + 1:hi], T.A[:, lo:hi - 1], T.Z[:, 1:n], B / K, OP.min, OP.max)
             if name == "behind":
-                return vec.tensor_tensor_scan(T.Suf[:, hi - 1:lo - 1 if lo else None:-1], T.A[:, a + n:a:-1], T.Z[:, 0:n], 0.0, OP.min, OP.max)
+                return vec.tensor_tensor_scan(T.Suf[:, hi - 2:lo - 1 if lo else None:-1], T.A[:, hi - 1:lo:-1], T.Z[:, 1:n], B / K, OP.min, OP.max)
             if name == "first":
-                return act.activation(T.Pre[:, lo:hi:8], T.Suf[:, lo:hi:8], AF.Copy)
+                o, i = T.Pre[:, lo:hi:8], T.Suf[:, lo:hi:8]
+                return vec.tensor_copy(o, i) if q == "V" else act.activation(o, i, AF.Copy)
             if name == "least":
                 return vec.tensor_tensor_scan(T.U[:, c], T.Suf[:, c], T.Pre[:, c], 0.0, OP.max, OP.min)
-            return vec.tensor_tensor_scan(T.Rc[:, c], T.S[:, c], T.U[:, c], 0.0, OP.add, OP.mult)
+            if name == "signed":
+                return vec.tensor_tensor_scan(T.Rc[:, c], T.S[:, c], T.U[:, c], 0.0, OP.add, OP.mult)
+            if name == "sum":
+                need("P", late["E32"], ("dr", 32))
+                run("P", ten.matmul(T.bk2[:, 0:80], T.E32[:, :], T.inva[:, :], True, False))
+                return ten.matmul(T.bk2[:, 0:80], T.E32[:, :], T.invb[:, :], False, True)
+            return vec.tensor_scalar(T.inv16[:, :], T.bk2[:, 0:80], 0.25 - OFF, 0.0, OP.add, OP.max)
 
-        todo = {q: list(CHECK[q]) for q in CHECK}
+        todo = {q: [t for t in CHECK[q] if not (r and t[0] in ("sum", "list"))] for q in CHECK}
         while any(todo.values()):
             for q in todo:
                 while todo[q]:
                     name, lo, hi = todo[q][0]
-                    if name == "list":
-                        if r == 0 and q == "P":
-                            need("P", late["E32"], ("dr", 32))
-                            run("P", ten.matmul(T.bk4[:, 0:80], T.E32[:, :], T.inva[:, :], True, False))
-                            inv[0] = run("P", ten.matmul(T.bk4[:, 0:80], T.E32[:, :], T.invb[:, :], False, True))
-                        elif r == 0:
-                            if not inv[0]:
-                                break
-                            need("V", inv[0])
-                            inv[0] = run("V", vec.tensor_scalar(T.inv16[:, :], T.bk4[:, 0:80], 0.25 - OFF, 0.0, OP.add, OP.max))
-                        todo[q].pop(0)
-                        continue
                     src = [[m for m in made[n] if m[0] < hi and lo < m[1]] for n in READS[name]]
                     if any(sum(min(hi, m[1]) - max(lo, m[0]) for m in ms) < hi - lo for ms in src):
                         break
                     todo[q].pop(0)
                     need(q, *[m[2] for ms in src for m in ms])
                     made[name].append((lo, hi, run(q, one(q, name, lo, hi))))
-        for d in (4, 1) if r else (RAW, 4, 1):
-            own_sign(dwin, d, ev[d])
-        sg = [bank(T["bk%d" % (5 + i)], 0) for i in range(2)]
-        for i in range(2 * r):
-            need("P", *late["got"])
-            run("P", ten.matmul(sg[i], T.NI[:, :], bank(T.Rv0, diff[i]), True, False))
-            t = run("P", ten.matmul(sg[i], eye, bank(T.Tg1, diff[i]), False, True))
-        dst = T["Rs%d" % r]
-        got = by_slots(2 * r + 1, T.Rc[:, 0:NJ], T.inv16, (dst, T["Lr%d" % r], T["Xr%d" % r], T["Rv%d" % r]),
+        inv[0] = inv[0] or made["list"][0][2]
+        got = by_slots(2 * r + 1, T.Rc[:, 0:NJ], T.inv16, (T["Rs%d" % r], T["Lr%d" % r], T["Xr%d" % r], T["Rv%d" % r]),
                        [made["signed"][-1][2], inv[0]])
-        for i in range(2 * r):
-            need("A", t)
-            sv[0] = run("A", act.activation(bank(T.sv1, i), sg[i], AF.Sign, bias=0.5))
-        if r:
-            need("P", sv[0])
+        for d in sg:
+            need("A", *sg[d][1])
+            sv[d] = run("A", act.activation(blk(T["sv%d" % r], d // 2), sg[d][0], AF.Sign))
         if r == 0:
-            for i in range(2):
-                so = run("A", act.activation(bank(T.so, i), bank(dwin, diff[i]), AF.Sign))
-            for i in range(2):
-                sv[0] = run("A", act.activation(bank(T.sv0, i), bank(T.Tg0, diff[i]), AF.Sign, bias=0.5))
-            need("V", vl_in, ("rn", LIST[1]))
+            so = [run("A", act.activation(blk(T.so, d // 2), blk(dwin, me ^ d), AF.Sign)) for d in LESS]
+            need("V", vl_in, ("rn", ON["rn"][1]))
             late["rn"] = run("V", vec.tensor_copy(T.rn16[:, :], T.rn32[:, :]))
             late["vl"] = run("V", vec.tensor_copy(T.vl16[:, :], T.vl32[:, :]))
-            need("V", so, *got.values())
-            for i in range(2):
-                rf[0] = run("V", vec.tensor_tensor_scan(bank(T.Rf, i), bank(T.so, i), bank(dst, diff[i]), 0.0, OP.add, OP.mult))
+            late["xk"] = run("V", vec.tensor_scalar(T.xk[:, :], T.xs[:, :], 0.5, 1 / K, OP.add, OP.mult))
+            late["so"] = so + list(got.values())
         return got[0]
 
     def variables(r, rs, out):
         rv = T["Rv%d" % r]
         ev = taken(2 * r + 1, T["Rs%d" % r], rs, T["Lr%d" % r], rv)
+        if r == 0:
+            need("V", *late["so"])
+            for d in LESS:
+                rf[d] = run("V", vec.tensor_tensor_scan(blk(T.Rf, d // 2), blk(T.so, d // 2), blk(T.Rs0, me ^ d), 0.0, OP.add, OP.mult))
         gd = T["Gv%d" % r]
-        need("V", late["vl"], *ev.values())
-        need("A", late["vl"], *ev.values())
 
-        def piece(d, lo=0, hi=256):
+        def piece(d, lo, hi):
             return gd[:, 256 * d + lo:256 * d + hi], rv[:, 0:W].indirect(T.vl16[:, 16 * d + lo // 16:16 * d + hi // 16])
 
         a, b, held, ins = (0, VA), (VA, V), {}, {}
-
-        def add(d, lo, hi):
-            o, i = piece(d, lo, hi)
-            if d:
-                need("V", held[lo][1])
-            held[lo] = (o, run("V", vec.tensor_tensor(o, i, held[lo][0] if d else T.xs[:, lo:hi], OP.add)))
-
-        need("P", ev[0])
+        tot = {lo: T["bk%d" % d][:, 0:hi - lo] for d, (lo, hi) in zip(FREE, (a, b))}
+        need("P", late["xk"], *sv.values())
+        for lo, hi in (a, b):
+            run("P", ten.matmul(tot[lo], eye, (T.xs if r else T.xk)[:, lo:hi], True, False))
+        need("V", late["vl"], *ev.values())
+        need("A", late["vl"], *ev.values())
         for d, (lo, hi), last in ((2, a, False), (3, a, True), (2, b, True)):
             o, i = piece(d, lo, hi)
             need("P", run("A", act.activation(o, i, AF.Copy)))
-            ins[lo] = run("P", ten.matmul(T["bk%d" % (lo > 0)][:, 0:hi - lo], eye, o, d == 2, last))
-        for d, part in ((0, b), (0, a), (1, b), (1, a), (3, b)):
-            add(d, *part)
+            ins[lo] = run("P", ten.matmul(tot[lo], eye, o, False, last))
+        for d, (lo, hi) in ((0, b), (0, a), (1, b), (1, a), (3, b)):
+            o, i = piece(d, lo, hi)
+            if d:
+                need("V", held[lo][1])
+            held[lo] = (o, run("V", vec.tensor_tensor(o, i, held[lo][0], OP.add) if d else vec.tensor_copy(o, i)))
         for lo, hi in (a, b):
             need("V", held[lo][1], ins[lo])
-            t = run("V", vec.tensor_tensor(out[:, lo:hi], T["bk%d" % (lo > 0)][:, 0:hi - lo], held[lo][0], OP.add))
+            t = run("V", vec.tensor_tensor(out[:, lo:hi], tot[lo], held[lo][0], OP.add))
+            if r:
+                q = "A" if lo else "S"
+                need(q, t)
+                t = move((T.ys, slice(lo, hi)), (T.y, slice(lo, hi)), kv, "dy", True, q + q)
         return t
 
     rs = check(0, own)
     tw = variables(0, rs, T.Tw)
     need("G", tw)
-    send_raw(2, T.Tw)
-    need("P", tw)
-    less_own((RAW, 7, 3, 2, 6))
-    got = by_slots(2, T.Tw[:, 0:256], T.sn16, (T.Tg1, T.Lm1, T.Xm1, T.Dw1), [tw])
+    send([(*PLAN[2]["calls"][0][0], T.Tw[:, :], [T.rx[:, :]], "arr2_%d" % me)])
+    need("P", tw, late["NI"])
+    for d in (*LESS, 4):
+        run("P", ten.matmul(ps(d), T.NI[:, :], blk(T.Rf, d // 2) if d % 2 else blk(T.Rs0, me ^ d), True, False))
+    got = by_slots(2, T.Tw[:, :], T.sn16, (T.Tg1, T.Lm1, T.Xm1, T.Dw1), [tw])
     late["got"] = list(got.values())
-    gather_raw(2)
+    need("V", late["rn"], arrived(2, RAW))
+    late["raw"] = run("V", vec.tensor_copy(blk(T.Lm1, me ^ RAW), T.rx[:, :].indirect(T.rn16[:, :])))
     rs = check(1, got[0])
     need("S", variables(1, rs, T.ys))
-    g.sync.dma_start(T.y[:, :], T.ys[:, :]).then_inc(T.sem.dy, 16)
-    need("S", ("dy", 16))
     for q in ("V", "A", "P", "G"):
         need("G", ("s" + q, cnt[q]))
     need("G", ("ls", cnt["ls"]))

from concourse.bass import DstId, RemoteDMATransfer
from concourse.mybir import dt, AluOpType, AxisListType, ActivationFunctionType

NR, CAP, V, M = 8, 160, 256, 128
W = NR * CAP
H = 4 * CAP
NJ = 8 * M
NH = NJ // 2
VA = 160
B = 51.0
K = float(2 ** 20)
BIG = float(2 ** 90)
OFF = 64
OP = AluOpType
AF = ActivationFunctionType
FREE = (2, 6)
AT_V = [4 * (p ^ 6) % 8 if p >= 4 else 0 for p in range(NR)]
AT_C = [(AT_V[q ^ 2] - q * (q ^ 2)) % 8 for q in range(NR)]
RAW = 5
OFFCHIP = 8
PART = {"g": (0, 10)}
FIRST = {"V": "x0 g2 x1 g7 x2 g4 x3 g0 c1", "A": "g3 g5 g1 n6 g6", "recv": "V0 A3 V7 A5 V4",
         "calls": [[(3, 0, 8), (2, 8, 8)], [(7, 0, 8)], [(5, 0, 8)], [(4, 0, 8)], [(1, 0, 4), (6, 4, 4)]]}
SECOND = {"V": "g2 g7 g1 g6 g0", "A": "g3 g4 c1 g5", "recv": "A0 s0 A5 A3 V7 A4",
          "calls": [[(5, 0, 8)], [(3, 0, 8), (2, 8, 8)], [(7, 0, 8)], [(4, 0, 8)], [(6, 0, 8)], [(1, 0, 8)]]}
TO_VARS = {"V": "g2 g4 g1 g0 g6", "A": "s2 s4 k2 s6 g3 g7 g5 k6 c4", "recv": "A0 V3 V7 V5 V1",
           "calls": [[(3, 0, 8), (2, 8, 8)], [(7, 0, 8)], [(5, 0, 8)], [(1, 0, 8)], [(4, 0, 4), (6, 4, 4)]]}
PLAN = {0: FIRST, 1: dict(TO_VARS, V="g2 g4 g1 g6 g0", A="s2 s4 s6 g3 g7 g5 c4 s0"), 2: SECOND, 3: TO_VARS}
ON = {"rn": (0, 8), 0: (0, 8), 1: (0, 8), 2: (0, 8), 3: (0, 8)}
LIST = (8, 8)
SV = 480
LESS = (3, 5)
READS = {"edges": [], "size": ["edges"], "product": ["edges"], "repeat": ["product"], "sign": ["repeat"],
         "before": ["size"], "behind": ["size"], "first": ["before", "behind"], "least": ["first"], "signed": ["least", "sign"],
         "sum": [], "list": ["sum"]}
H0, H1, ALL = (0, NH), (NH, NJ), (0, NJ)
Q0, Q1, Q2, Q3 = (0, 256), (256, NH), (NH, 864), (864, NJ)
CHECK = {"V": [("edges", 0, 288), ("edges", 512, 640), ("product", *H0), ("edges", 640, 768), ("behind", *Q0), ("before", *Q0), ("product", *H1)]
         + [(n, *q) for q in (Q1, Q2) for n in ("behind", "before")] + [("before", *Q3), ("behind", *Q3)]
         + [("least", *H0), ("first", *Q3), ("least", *Q2), ("least", *Q3), ("signed", *H0), ("list", *ALL), ("signed", *H1)],
         "A": [("edges", 288, 512), ("edges", 768, 928), ("size", *Q0), ("edges", 928, NJ), ("size", *Q1), ("size", *Q2), ("size", *Q3),
               ("sign", *Q0), ("first", *H0), ("sign", *Q1), ("first", *Q2), ("sign", *H1)],
         "P": [("repeat", *H0), ("repeat", *H1), ("sum", *ALL)]}

SCRATCH = {
    "sn32": ("sbuf", [128, 80], "int32"), "pl32": ("sbuf", [128, 64], "int32"), "vl32": ("sbuf", [128, 64], "int32"),
    "sn16": ("sbuf", [128, 80], "uint16"), "pl16": ("sbuf", [128, 64], "uint16"), "vl16": ("sbuf", [128, 64], "uint16"),
    "pm32": ("sbuf", [128, 64], "int32"), "ln32": ("sbuf", [128, 10], "int32"), "rn32": ("sbuf", [128, 10], "int32"),
    "rn16": ("sbuf", [128, 10], "uint16"), "hl": ("sbuf", [128, 10], "int32"), "hx": ("sbuf", [128, 4 * CAP], "bfloat16"),
    "hd": ("dram", [4 * 256, CAP], "bfloat16"),
    "ta": ("sbuf", [128, 64], "int32"), "tb": ("sbuf", [128, 64], "int32"), "tc": ("sbuf", [128, 64], "int32"),
    "td": ("sbuf", [128, 64], "int32"), "pc16": ("sbuf", [128, 64], "uint16"),
    "num": ("sbuf", [128, NJ], "float32"),
    "iva": ("sbuf", [128, W], "float32"), "ivb": ("sbuf", [128, W], "float32"),
    "inva": ("sbuf", [128, 80], "float32"), "invb": ("sbuf", [128, 80], "float32"), "nil": ("sbuf", [128, 320], "float32"),
    "inv16": ("sbuf", [128, 80], "uint16"),
    "E": ("sbuf", [128, 256], "bfloat16"), "NI": ("sbuf", [128, 128], "bfloat16"),
    "EK": ("sbuf", [128, 256], "bfloat16"), "E32": ("sbuf", [128, 128], "float32"),
    "xs": ("sbuf", [128, V], "bfloat16"), "xk": ("sbuf", [128, V], "bfloat16"), "Tw": ("sbuf", [128, V], "bfloat16"),
    "rx": ("sbuf", [128, V], "bfloat16"), "ys": ("sbuf", [128, V], "float32"),
    "Z": ("sbuf", [128, NH], "bfloat16"), "Zf": ("sbuf", [128, NH], "bfloat16"),
}
for _n in ("D", "A", "F", "Pre", "Suf", "S", "U", "Rc"):
    SCRATCH[_n] = ("sbuf", [128, NJ], "bfloat16")
for _n in ("sc", "sk", "so", "Rf"):
    SCRATCH[_n] = ("sbuf", [128, H], "bfloat16")
for _d in range(NR):
    SCRATCH["bk%d" % _d] = ("psum", [128, 512], "float32")
for _r in range(2):
    for _n, _w in (("Tg", W), ("Rs", W), ("Lm", W), ("Lr", W), ("Xm", W), ("Xr", W), ("Dw", W), ("Rv", W), ("Gv", 1024), ("sv", H)):
        SCRATCH["%s%d" % (_n, _r)] = ("sbuf", [128, _w], "bfloat16")
SEMAPHORES = ["sV", "sA", "sP", "sG", "dl", "dx", "dpm", "dsn", "dpl", "dvl", "df", "dr", "dy", "ls", "rn", "hl"]
SEMAPHORES += ["arr%d_%d" % (ph, p) for ph in range(4) for p in range(NR)] + ["hop%d" % ph for ph in range(4)]


def blk(buf, q):
    return buf[:, q * CAP:(q + 1) * CAP]


def helper(topo, cores, c):
    return [h for h in topo.cores_of(c) if topo.die(h) != topo.die(c) and all(topo.may_write(h, o) for o in cores)][0]


def shift(ph, src, dst):
    p, q = (dst, src) if ph % 2 else (src, dst)
    return (p * q + AT_C[q] - AT_V[p]) * (-1 if ph % 2 else 1) % 8


def handed(ph):
    return [d for call in PLAN[ph]["calls"] for d, o, n in call if o >= OFFCHIP][0]


def hop(T, ph, r):
    k = shift(ph, r, r ^ handed(ph))
    if not k:
        return [blk(T.hx, ph)], blk(T.hx, ph)
    o = 256 * ph
    return [T.hd[o:o + 128, :], T.hd[o + 128:o + 256, :]], T.hd[o + 128 - 16 * k:o + 256 - 16 * k, :]


def hand_on(g, core, T, topo, r):
    jobs = [(RAW, T.hl[:, :], "hl", LIST[1], T.rn32[:, :], "rn", ON["rn"])]
    for ph in range(4):
        there, on = hop(T, ph, r)
        jobs.append((handed(ph), on, "hop%d" % ph, 8 * len(there), blk(T[("Dw%d", "Rv%d")[ph % 2] % (ph // 2)], r), "arr%d_%d" % (ph, r), ON[ph]))
    for d, src, sem, n, dst, arr, (o, k) in jobs:
        to = T.cores[r ^ d]
        rid, pid, _s = topo.addr(to)
        g.wait_ge(T.sem[sem], n)
        g.remote_dma(dst, src, T.sem[arr], T.sem.ls, pid, rid, sum(1 << e for e in topo.engines(core, to)[o:o + k]))
    g.wait_ge(T.sem.ls, sum(j[-1][1] for j in jobs))


def rank_program(g, core, T, topo):
    me = T.rank_of(core)
    if me is None:
        for r, c in enumerate(T.cores):
            if helper(topo, T.cores, c) == core:
                hand_on(g, core, T, topo, r)
        return
    queue = {"V": g.vector, "A": g.scalar, "P": g.tensor, "G": g, "S": g.sync}
    cnt = {"V": 0, "A": 0, "P": 0, "G": 0, "ls": 0}
    seen = {}
    vec, act, ten = g.vector, g.scalar, g.tensor

    def need(q, *toks):
        for sem, val in toks:
            if seen.get((q, sem), 0) < val:
                queue[q].wait_ge(T.sem[sem], val)
                seen[(q, sem)] = val

    def run(q, inst):
        cnt[q] += 1
        inst.then_inc(T.sem["s" + q], 1)
        return ("s" + q, cnt[q])

    def ps(d):
        return T["bk%d" % d][:, 0:CAP]

    def turn(ph, r, sender):
        s = (128 - 16 * (shift(ph, me, r) if sender else shift(ph, r, me))) % 128
        return (T.EK if ph == 3 else T.E)[:, s:s + 128]

    def move(sb, hbm, k, sem, store=False, queues="SS", rows=lambda a, b: slice(a, b)):
        for q, (a, b, o) in zip(queues, ((0, 128 - 16 * k, 16 * k), (128 - 16 * k, 128, 16 * k - 128))):
            if a < b:
                sides = sb[0][a + o:b + o, sb[1]], hbm[0][rows(a, b), hbm[1]]
                queue[q].dma_start(*sides[::-1] if store else sides).then_inc(T.sem[sem], 16)
                cnt[sem] = cnt.get(sem, 0) + 16
        return (sem, cnt[sem])

    def places(i):
        need("V", pc[0] or pl_in)
        if i == 0:
            run("V", vec.tensor_scalar(T.ta[:, :], T.pl32[:, :], 15, None, OP.bitwise_and))
            pc[0] = run("V", vec.tensor_scalar(T.tb[:, :], T.pl32[:, :], 4, None, OP.arith_shift_right))
        elif i == 1:
            pc[0] = run("V", vec.tensor_scalar(T.tc[:, :], T.ta[:, :], 80.0, None, OP.mult))
        elif i == 2:
            pc[0] = run("V", vec.tensor_tensor(T.td[:, :], T.tc[:, :], T.tb[:, :], OP.add))
        else:
            pc[0] = run("V", vec.tensor_copy(T.pc16[:, :], T.td[:, :]))

    eye, pc, whole, kv, kc = T.E[:, 0:128], [None], slice(None), AT_V[me], AT_C[me]
    ln_in = move((T.ln32, whole), (T.sn, slice((me ^ RAW) * 10, (me ^ RAW) * 10 + 10)), kv, "dl", queues="AA")
    sn_in = move((T.sn32, whole), (T.sn, whole), kv, "dsn")
    pl_in = move((T.pl32, whole), (T.pl, whole), kc, "dpl", queues="AA")
    x_in = move((T.xs, whole), (T.x, whole), kv, "dx")
    num = run("G", g.iota(T.num[:, 0:256], [[1, 2], [8, 16], [128, 8]], OFF, 0, allow_small_or_imprecise_dtypes=True))
    z = [run("V", vec.memset(T.Zf[:, :], -BIG))]
    need("A", *z)
    z = [run("A", act.activation(T.Zf[:, 0:NH:8], T.Zf[:, 0:NH:8], AF.Silu, scale=-1.0))]
    fill = run("V", vec.memset(T.nil[:, :], 0.0))
    need("G", fill)
    eyes = run("G", g.affine_select(T.E[:, :], T.nil[:, 0:256], [[0, 2], [-1, 128]], OP.not_equal, 1.0, 0, 1))
    for u in range(8):
        if u == 3:
            need("S", fill)
            for win in (T.iva, T.ivb):
                g.sync.dma_start(win[0:128:16, :], T.nil[0:32, :]).then_inc(T.sem.df, 16)
        pm_in = move((T.pm32, slice(8 * u, 8 * u + 8)), (T.pl, whole), kc, "dpm", rows=lambda a, b: slice(a + u, b, 8))
    z.append(run("V", vec.memset(T.Suf[:, 7:NJ:8], B / K)))
    need("V", num)
    for e in (2, 4):
        num = run("V", vec.tensor_scalar(T.num[:, 128 * e:128 * e + 256], T.num[:, 0:256], float(e), None, OP.add))
    need("V", sn_in)
    sn16 = run("V", vec.tensor_copy(T.sn16[:, :], T.sn32[:, :]))

    def toks(ph, name, kind=None):
        return [(t[0], int(t[1:])) for t in PLAN[ph][name].split() if kind is None or t[0] == kind]

    def turned_here(ph):
        return [d for q in "VA" for k, d in toks(ph, q, "c")]

    def arrived(ph, d):
        return ("arr%d_%d" % (ph, me ^ d), [n if o < OFFCHIP else ON[ph][1] for c in PLAN[ph]["calls"] for e, o, n in c if e == d][0])

    def send(items):
        tr = []
        for d, o, n, src, dst, sem in items:
            to = T.cores[me ^ d] if o + n <= OFFCHIP else helper(topo, T.cores, core)
            rid, pid, _s = topo.addr(to)
            tr.append(RemoteDMATransfer(dst_ids=[DstId(rid=rid, pnc=pid)] * len(dst), remote_sem=T.sem[sem], src=src, dsts=dst,
                                        dma_engine_mask=sum(1 << e for e in topo.engines(core, to)[o:o + n])))
            cnt["ls"] += n
        g.remote_dma_fused(tr, local_sem=T.sem.ls)

    def drain(q, out, src):
        return run("V", vec.tensor_copy(out, src)) if q == "V" else run("A", act.activation(out, src, AF.Copy))

    def by_slots(ph, win, lst, bufs, ready):
        src, land, xsrc, xland = bufs
        xs, got, out, trn = turned_here(ph), {}, {}, {}

        def gather(q, d, lo, hi):
            r = me ^ d
            need(q, *ready)
            i, o = win.indirect(lst[:, r * 10 + lo:r * 10 + hi]), src[:, r * CAP + 16 * lo:r * CAP + 16 * hi]
            if ph == 0:
                if q == "A":
                    return run("A", act.activation(o, i, AF.Identity, bias=0.5 / K, scale=1 / K))
                return run("V", vec.tensor_scalar(o, i, 0.5, 1 / K, OP.add, OP.mult))
            if q == "A":
                return run("A", act.activation(o, i, AF.Copy))
            if ph == 2:
                return run("V", vec.tensor_tensor(o, i, blk(T.Rv0, r), OP.subtract))
            if d % 2 == 0:
                need("V", sc[d])
                return run("V", vec.tensor_tensor(o, i, blk(T.sk if ph == 3 and d in (*FREE, handed(ph)) else T.sc, d // 2), OP.mult))
            return run("V", vec.tensor_copy(o, i))

        todo = {q: toks(ph, q) for q in "VA"}
        while todo["V"] or todo["A"]:
            for q in "VA":
                while todo[q]:
                    kind, d = todo[q][0]
                    if d not in trn if kind == "c" else q == "V" and ph % 2 and d % 2 == 0 and (d not in sc or ("k", d) in todo["A"]):
                        break
                    todo[q].pop(0)
                    r = me ^ d
                    if kind == "n":
                        need("A", num)
                        late["num"] = run("A", act.activation(T.num[:, 128 * d:NJ], T.num[:, 0:256], AF.Identity, bias=float(d)))
                    elif kind == "x":
                        places(d)
                    elif kind == "s":
                        own_sign(T["Dw%d" % (ph // 2)], d, late["ev"][d])
                    elif kind == "k":
                        times_k(d)
                    elif kind == "c":
                        need(q, trn[d])
                        out[d] = drain(q, blk(xsrc, r), ps(d))
                    else:
                        got[d] = out[d, kind] = gather(q, d, *PART[kind])
                        if d in xs:
                            need("P", late["EK"] if ph == 3 else eyes, got[d])
                            trn[d] = run("P", ten.matmul(ps(d), turn(ph, r, True), blk(src, r), True, True))
        for c in PLAN[ph]["calls"][int(ph == 2):]:
            need("G", *[out[k] for d, o, n in c for k in ([d] if d in xs else [(d, part) for part in PART]) if k in out])
            send([(d, o, n, blk(xsrc if d in xs else src, me ^ d),
                   *((hop(T, ph, me)[0], "hop%d" % ph) if o >= OFFCHIP else ([blk(xland if d in xs or d in FREE else land, me)], "arr%d_%d" % (ph, me))))
                  for d, o, n in c])
        return got

    def own_sign(dwin, d, there):
        need("A", there)
        sc[d] = run("A", act.activation(blk(T.sc, d // 2), blk(dwin, me ^ d), AF.Sign))

    def times_k(d):
        need("A", sc[d])
        sc[d] = run("A", act.activation(blk(T.sk, d // 2), blk(T.sc, d // 2), AF.Identity, scale=K))

    def taken(ph, mine, mine_ready, land, rv):
        done, ev = {}, {}
        for q, d in [t for t in toks(ph, "recv") if t[0] != "s"]:
            p = me ^ d
            need("P", late["EK"] if ph == 3 else eyes, late["raw"] if (ph, d) == (2, RAW) else arrived(ph, d) if d else mine_ready)
            done[d] = run("P", ten.matmul(ps(d), turn(ph, p, False), blk(land if d else mine, p), not (ph == 2 and d in (4, *LESS)), True))
        for q, d in toks(ph, "recv"):
            p = me ^ d
            if q == "s":
                own_sign(rv, d, ev[d])
                continue
            need(q, done[d])
            if ph % 2 and d % 2:
                need("V", sv[d])
                ev[d] = run("V", vec.tensor_tensor(blk(rv, p), ps(d), blk(T["sv%d" % (ph // 2)], d // 2), OP.mult))
            else:
                ev[d] = drain(q, blk(rv, p), ps(d))
        for d in (*turned_here(ph), *FREE, handed(ph)):
            ev[d] = arrived(ph, d)
        return ev

    inv, rf, sv, sc, late = [None], {}, {}, {}, {}
    need("G", ln_in)
    send([(RAW, *LIST, T.ln32[:, :], [T.hl[:, :]], "hl")])
    own = by_slots(0, T.xs[:, :], T.sn16, (T.Tg0, T.Lm0, T.Xm0, T.Dw0), [sn16, x_in])[0]
    need("V", pc[0], num, ("df", 32))
    scat = run("V", vec.tensor_copy(T.iva[:, 0:W].indirect(T.pc16[:, 0:SV // 16]), T.num[:, 0:SV]))
    for a in (0, 256):
        z.append(run("G", g.affine_select(T.Z[:, a:a + 256], T.nil[:, 0:256], [[0, 32], [1, 8]], OP.not_equal, B / K, 0, 0)))
    for o, n, s in ((T.E32, 1, 1.0), (T.NI, 1, -1.0), (T.EK, 2, K)):
        late[o.name] = run("G", g.affine_select(o[:, :], T.nil[:, 0:128 * n], [[0, n], [-1, 128]], OP.not_equal, s, 0, 1))
    need("A", pc[0], late["num"], ("df", 32))
    scat2 = run("A", act.activation(T.ivb[:, 0:W].indirect(T.pc16[:, SV // 16:64]), T.num[:, SV:NJ], AF.Silu))
    need("S", scat)
    g.sync.dma_start(T.inva[:, :], T.iva[0:128:16, :]).then_inc(T.sem.dr, 16)
    need("S", scat2)
    g.sync.dma_start(T.invb[:, :], T.ivb[0:128:16, :]).then_inc(T.sem.dr, 16)
    vl_in = move((T.vl32, whole), (T.vl, whole), kv, "dvl")
    need("V", pm_in)
    pl16 = run("V", vec.tensor_copy(T.pl16[:, :], T.pm32[:, :]))

    def check(r, mine_ready):
        dwin = T["Dw%d" % r]
        sc.clear()
        ev = late["ev"] = taken(2 * r, T["Tg%d" % r], mine_ready, T["Lm%d" % r], dwin)
        win = dwin[:, 0:W]
        need("V", pl16, *ev.values())
        need("A", pl16, *ev.values())
        need("V", *z)
        sg = {d: (blk(T["Tg%d" % r], me ^ d), []) for d in (3, 7, 5, 1)}
        for i, d in enumerate(LESS * r):
            need("P", *late["got"])
            run("P", ten.matmul(ps(FREE[i]), T.NI[:, :], blk(T.Rv0, me ^ d), True, False))
            sg[d] = ps(FREE[i]), [run("P", ten.matmul(ps(FREE[i]), eye, blk(T.Tg1, me ^ d), False, True))]
        made = {n: [] for n in READS}

        def one(q, name, lo, hi):
            c, n = slice(lo, hi), hi - lo
            if name == "edges":
                o, i = T.D[:, c], win.indirect(T.pl16[:, lo // 16:hi // 16])
                return vec.tensor_copy(o, i) if q == "V" else act.activation(o, i, AF.Copy)
            if name == "size":
                return act.activation(T.A[:, c], T.D[:, c], AF.Abs, bias=-0.5 / K)
            if name == "product":
                return vec.tensor_tensor_scan(T.F[:, c], T.Zf[:, 0:n], T.D[:, c], 0.0, OP.max, OP.mult)
            rep = T["bk%d" % (3 + lo // NH)]
            if name == "repeat":
                for e in range(7):
                    run("P", ten.matmul(rep[:, e:NH:8], eye, T.F[:, lo + 7:hi:8], True, True))
                return ten.matmul(rep[:, 7:NH:8], eye, T.F[:, lo + 7:hi:8], True, True)
            if name == "sign":
                return act.activation(T.S[:, c], rep[:, lo % NH:lo % NH + n], AF.Sign)
            if name == "before":
                return vec.tensor_tensor_scan(T.Pre[:, lo + 1:hi], T.A[:, lo:hi - 1], T.Z[:, 1:n], B / K, OP.min, OP.max)
            if name == "behind":
                return vec.tensor_tensor_scan(T.Suf[:, hi - 2:lo - 1 if lo else None:-1], T.A[:, hi - 1:lo:-1], T.Z[:, 1:n], B / K, OP.min, OP.max)
            if name == "first":
                o, i = T.Pre[:, lo:hi:8], T.Suf[:, lo:hi:8]
                return vec.tensor_copy(o, i) if q == "V" else act.activation(o, i, AF.Copy)
            if name == "least":
                return vec.tensor_tensor_scan(T.U[:, c], T.Suf[:, c], T.Pre[:, c], 0.0, OP.max, OP.min)
            if name == "signed":
                return vec.tensor_tensor_scan(T.Rc[:, c], T.S[:, c], T.U[:, c], 0.0, OP.add, OP.mult)
            if name == "sum":
                need("P", late["E32"], ("dr", 32))
                run("P", ten.matmul(T.bk2[:, 0:80], T.E32[:, :], T.inva[:, :], True, False))
                return ten.matmul(T.bk2[:, 0:80], T.E32[:, :], T.invb[:, :], False, True)
            return vec.tensor_scalar(T.inv16[:, :], T.bk2[:, 0:80], 0.25 - OFF, 0.0, OP.add, OP.max)

        todo = {q: [t for t in CHECK[q] if not (r and t[0] in ("sum", "list"))] for q in CHECK}
        while any(todo.values()):
            for q in todo:
                while todo[q]:
                    name, lo, hi = todo[q][0]
                    src = [[m for m in made[n] if m[0] < hi and lo < m[1]] for n in READS[name]]
                    if any(sum(min(hi, m[1]) - max(lo, m[0]) for m in ms) < hi - lo for ms in src):
                        break
                    todo[q].pop(0)
                    need(q, *[m[2] for ms in src for m in ms])
                    made[name].append((lo, hi, run(q, one(q, name, lo, hi))))
        inv[0] = inv[0] or made["list"][0][2]
        got = by_slots(2 * r + 1, T.Rc[:, 0:NJ], T.inv16, (T["Rs%d" % r], T["Lr%d" % r], T["Xr%d" % r], T["Rv%d" % r]),
                       [made["signed"][-1][2], inv[0]])
        for d in sg:
            need("A", *sg[d][1])
            sv[d] = run("A", act.activation(blk(T["sv%d" % r], d // 2), sg[d][0], AF.Sign))
        if r == 0:
            so = [run("A", act.activation(blk(T.so, d // 2), blk(dwin, me ^ d), AF.Sign)) for d in LESS]
            need("V", vl_in, ("rn", ON["rn"][1]))
            late["rn"] = run("V", vec.tensor_copy(T.rn16[:, :], T.rn32[:, :]))
            late["vl"] = run("V", vec.tensor_copy(T.vl16[:, :], T.vl32[:, :]))
            late["xk"] = run("V", vec.tensor_scalar(T.xk[:, :], T.xs[:, :], 0.5, 1 / K, OP.add, OP.mult))
            late["so"] = so + list(got.values())
        return got[0]

    def variables(r, rs, out):
        rv = T["Rv%d" % r]
        ev = taken(2 * r + 1, T["Rs%d" % r], rs, T["Lr%d" % r], rv)
        if r == 0:
            need("V", *late["so"])
            for d in LESS:
                rf[d] = run("V", vec.tensor_tensor_scan(blk(T.Rf, d // 2), blk(T.so, d // 2), blk(T.Rs0, me ^ d), 0.0, OP.add, OP.mult))
        gd = T["Gv%d" % r]

        def piece(d, lo, hi):
            return gd[:, 256 * d + lo:256 * d + hi], rv[:, 0:W].indirect(T.vl16[:, 16 * d + lo // 16:16 * d + hi // 16])

        a, b, held, ins = (0, VA), (VA, V), {}, {}
        tot = {lo: T["bk%d" % d][:, 0:hi - lo] for d, (lo, hi) in zip(FREE, (a, b))}
        need("P", late["xk"], *sv.values())
        for lo, hi in (a, b):
            run("P", ten.matmul(tot[lo], eye, (T.xs if r else T.xk)[:, lo:hi], True, False))
        need("V", late["vl"], *ev.values())
        need("A", late["vl"], *ev.values())
        for d, (lo, hi), last in ((2, a, False), (3, a, True), (2, b, True)):
            o, i = piece(d, lo, hi)
            need("P", run("A", act.activation(o, i, AF.Copy)))
            ins[lo] = run("P", ten.matmul(tot[lo], eye, o, False, last))
        for d, (lo, hi) in ((0, b), (0, a), (1, b), (1, a), (3, b)):
            o, i = piece(d, lo, hi)
            if d:
                need("V", held[lo][1])
            held[lo] = (o, run("V", vec.tensor_tensor(o, i, held[lo][0], OP.add) if d else vec.tensor_copy(o, i)))
        for lo, hi in (a, b):
            need("V", held[lo][1], ins[lo])
            t = run("V", vec.tensor_tensor(out[:, lo:hi], tot[lo], held[lo][0], OP.add))
            if r:
                q = "A" if lo else "S"
                need(q, t)
                t = move((T.ys, slice(lo, hi)), (T.y, slice(lo, hi)), kv, "dy", True, q + q)
        return t

    rs = check(0, own)
    tw = variables(0, rs, T.Tw)
    need("G", tw)
    send([(*PLAN[2]["calls"][0][0], T.Tw[:, :], [T.rx[:, :]], "arr2_%d" % me)])
    need("P", tw, late["NI"])
    for d in (*LESS, 4):
        run("P", ten.matmul(ps(d), T.NI[:, :], blk(T.Rf, d // 2) if d % 2 else blk(T.Rs0, me ^ d), True, False))
    got = by_slots(2, T.Tw[:, :], T.sn16, (T.Tg1, T.Lm1, T.Xm1, T.Dw1), [tw])
    late["got"] = list(got.values())
    need("V", late["rn"], arrived(2, RAW))
    late["raw"] = run("V", vec.tensor_copy(blk(T.Lm1, me ^ RAW), T.rx[:, :].indirect(T.rn16[:, :])))
    rs = check(1, got[0])
    need("S", variables(1, rs, T.ys))
    for q in ("V", "A", "P", "G"):
        need("G", ("s" + q, cnt[q]))
    need("G", ("ls", cnt["ls"]))
